import numpy as np
import ml_dtypes


def mxq(x, axis, fmt="e4m3"):
    dtype, down = {"e4m3": (ml_dtypes.float8_e4m3fn, 7), "e5m2": (ml_dtypes.float8_e5m2, 14)}[fmt]
    v = np.moveaxis(np.asarray(x, np.float32).astype(ml_dtypes.bfloat16).astype(np.float64), axis, -1)
    blocks = v.reshape(v.shape[:-1] + (-1, 32))
    amax = np.abs(blocks).max(-1, keepdims=True)
    byte = np.maximum(np.where(amax > 0, np.frexp(amax)[1] - 1 + 127, 0) - down, 1)
    scale = np.exp2(byte - 127.0)
    codes = (blocks / scale).astype(np.float32).astype(dtype).astype(np.float64)
    return np.moveaxis((codes * scale).reshape(v.shape), -1, axis)


WIDE = False


def mx_kscale(k):
    if not WIDE:
        return np.ones(k)
    levels = np.array([10, -10, 5, -5, 0])
    if k % 512:
        return np.exp2(np.random.permutation(np.resize(levels, k // 32))).repeat(32)
    a = np.empty((k // 512, 16))
    for p in range(k // 512):
        a[p, :8] = np.random.permutation(np.resize(levels, 8))
        for g in range(8):
            far = levels[np.abs(levels - a[p, g]) >= 10]
            a[p, g + 8] = far[np.random.randint(len(far))]
    return np.exp2(a.ravel()).repeat(32)


BF16 = ml_dtypes.bfloat16


def bf(x):
    return np.asarray(x, np.float32).astype(BF16)


def f64(x):
    return np.asarray(x).astype(np.float64)


E2M1 = np.array([0.0, 0.5, 1.0, 1.5, 2.0, 3.0, 4.0, 6.0, -0.0, -0.5, -1.0, -1.5, -2.0, -3.0, -4.0, -6.0])


def pack_weight(w, fmt):
    k, n = w.shape
    w = f64(bf(w)).reshape(k // 32, 32, n)
    amax = np.abs(w).max(1)
    if fmt == "e4m3":
        byte = np.frexp(amax)[1] - 1 + 127 - 7
    else:
        mant, ex = np.frexp(amax / 6.0)
        byte = np.where(mant > 0.5, ex, ex - 1) + 127
    byte = np.clip(np.where(amax > 0, byte, 1), 1, 254)
    scaled = (w * np.exp2(127.0 - byte)[:, None, :]).reshape(k, n).astype(np.float32)
    by_word = np.ascontiguousarray(scaled.reshape(k // 512, 128, 4, n).transpose(0, 1, 3, 2))
    if fmt == "e4m3":
        words = by_word.astype(ml_dtypes.float8_e4m3fn).view(np.uint8)
    else:
        c = by_word.astype(ml_dtypes.float4_e2m1fn).view(np.uint8) & 0xF
        words = c[..., 0::2] | (c[..., 1::2] << 4)
    return np.ascontiguousarray(words), np.ascontiguousarray(byte.astype(np.uint8).reshape(k // 512, 16, n))


def unpack_weight(words, scales, fmt):
    g, p, n, _ = words.shape
    if fmt == "e4m3":
        vals = np.ascontiguousarray(words).view(ml_dtypes.float8_e4m3fn).astype(np.float64)
    else:
        nib = np.empty((g, p, n, 4), np.uint8)
        nib[..., 0::2] = words & 0xF
        nib[..., 1::2] = words >> 4
        vals = E2M1[nib]
    vals = vals * np.repeat(np.exp2(scales.astype(np.float64) - 127.0), 8, axis=1)[..., None]
    return vals.transpose(0, 1, 3, 2).reshape(g * 512, n)
def pack4(w):
    words, scales = pack_weight(w, "e2m1")
    return words.reshape(words.shape[0], 128, -1), scales


def unpack4(words, scales):
    return unpack_weight(words.reshape(words.shape[0], 128, -1, 2), scales, "e2m1")


def planes(Y):
    n, m = Y.shape
    b = f64(bf(Y)).reshape(n // 32, 32, m)
    amax = np.abs(b).max(1)
    byte = np.clip(np.where(amax > 0, np.frexp(amax)[1] - 1 + 127 - 7, 1), 1, 254)
    codes = (b * np.exp2(127.0 - byte)[:, None, :]).reshape(n, m).astype(np.float32).astype(ml_dtypes.float8_e4m3fn).view(np.uint8)
    words = codes.reshape(n // 512, 128, 4, m).transpose(0, 1, 3, 2)
    return np.ascontiguousarray(words), np.ascontiguousarray(byte.astype(np.uint8).reshape(n // 512, 16, m))


D, UNITS, KN, KO, R, I = 1024, 1536, 512, 1024, 1024, 512

def positive(sigma, *shape):
    return np.exp(sigma * np.random.randn(*shape) - 0.5 * sigma * sigma)

def setup_inputs():
    s_now, s_old, s_in = mx_kscale(KN), mx_kscale(KO), mx_kscale(I)
    t = mx_kscale(R)
    mix_now = positive(1.2, D, KN) * s_now
    profiles_now = 0.5 * positive(1.0, KN, R) / KN / s_now[:, None] * t
    mix_old = positive(1.2, D, KO) * s_old
    profiles_old = 0.5 * positive(1.0, KO, R) / KO / s_old[:, None] * t
    profiles_old_words, profiles_old_scales = pack4(profiles_old)
    floor_weight = 0.2 * positive(0.5, R) * t
    outputs = positive(1.0, R, UNITS) * positive(0.4, UNITS) / R / t[:, None]
    input_weights = positive(1.2, D, I) * s_in
    inputs = positive(1.0, I, UNITS) * positive(0.3, UNITS) / I / s_in[:, None]
    intercept = 0.3 * positive(0.5, D)
    vote = np.exp(0.8 * np.random.randn(D))
    return {"mix_now": bf(mix_now), "profiles_now": bf(profiles_now), "mix_old": bf(mix_old),
            "profiles_old_words": profiles_old_words, "profiles_old_scales": profiles_old_scales,
            "floor_weight": bf(floor_weight), "outputs": bf(outputs), "input_weights": bf(input_weights),
            "inputs": bf(inputs), "intercept": bf(intercept), "vote": bf(vote)}

def reference(mix_now, profiles_now, mix_old, profiles_old_words, profiles_old_scales, floor_weight,
              outputs, input_weights, inputs, intercept, vote):
    now = mxq(f64(mix_now), 1) @ mxq(f64(profiles_now), 0)
    old = mxq(f64(mix_old), 1) @ unpack4(profiles_old_words, profiles_old_scales)
    U = now + old + f64(floor_weight)[None, :]
    weighted_out = mxq(U, 1) @ mxq(f64(outputs), 0)
    weighted_in = mxq(f64(input_weights), 1) @ mxq(f64(inputs), 0)
    y = f64(vote)[:, None] * (weighted_out + f64(intercept)[:, None]) / weighted_in
    Y = y.reshape(D, UNITS)
    words, scales = planes(Y)
    return y, words, scales

@@ -1,0 +1,407 @@
+from contextlib import ExitStack
+
+import concourse.mybir as mybir
+from concourse.masks import make_identity
+
+D, UNITS, KN, KO, R, I = 1024, 1536, 512, 1024, 1024, 512
+FLOPS = 2 * D * R * (KN + KO) + 2 * D * UNITS * (R + I)
+
+F32 = mybir.dt.float32
+BF16 = mybir.dt.bfloat16
+I32 = mybir.dt.int32
+U32 = mybir.dt.uint32
+U8 = mybir.dt.uint8
+FP8X4 = mybir.dt.float8_e4m3fn_x4
+FP4X4 = mybir.dt.float4_e2m1fn_x4
+ACT = mybir.ActivationFunctionType
+ALU = mybir.AluOpType
+
+P = 128
+PACK = 4
+SPAN = P * PACK
+WIDE = SPAN * PACK
+GROUPS = D // SPAN
+CHUNKS = UNITS // SPAN
+AHEAD = 8
+LOADS = [("in", 0, 0), ("iw", 0, 0), ("pn", 0, 0), ("mn", 0, 0), ("old", 0, 0), ("mo", 0, 0), ("pn", 1, 0), ("mo", 0, 1), ("in", 0, 1), ("out", 0, 0), ("out", 1, 0), ("out", 0, 1), ("mn", 1, 0), ("mo", 1, 0), ("mo", 1, 1), ("out", 1, 1), ("in", 0, 2), ("iw", 1, 0), ("out", 0, 2), ("out", 1, 2)]
+SHARE = 64
+YSHARE = 32
+LEAD = 4
+
+
+def tile_cross_efficiency_composed_weights_k6_kernel(
+    tc, mix_now, profiles_now, mix_old, old_words, old_scales, floor_weight,
+    outputs, input_weights, inputs, intercept, vote, out_0, out_1, out_2,
+):
+    nc = tc.nc
+    with ExitStack() as ctx:
+        keep = ctx.enter_context(tc.tile_pool(name="keep", bufs=1))
+        work = ctx.enter_context(tc.tile_pool(name="work", bufs=2))
+        psum = ctx.enter_context(tc.psum_pool(name="psum", bufs=8))
+
+        def span(i):
+            return slice(i * SPAN, (i + 1) * SPAN)
+
+        def part(i):
+            return slice(i * P, (i + 1) * P)
+
+        def bank():
+            return psum.tile([P, SPAN], F32, name="bank", tag="bank", bufs=5)
+
+        def staged():
+            return work.tile([P, WIDE], BF16, name="staged", tag="staged", bufs=6, align_bytes=64)
+
+        raw, packed, stage = {}, {}, {}
+
+        identity = keep.tile([P, P], F32, name="identity")
+        make_identity(nc, identity[:])
+        old_scale_rows = keep.tile([P, 2 * R], U8, name="old_scale_rows")
+        nc.gpsimd.memset(old_scale_rows[:].bitcast(I32), 0)
+        floor_spread = keep.tile([P, 2 * P], F32, name="floor_spread")
+        nc.gpsimd.memset(floor_spread[:], 0.0)
+
+        vote_cols = keep.tile([P, GROUPS * PACK], BF16, name="vote_cols")
+        intercept_cols = keep.tile([P, GROUPS * PACK], BF16, name="intercept_cols")
+        floor_rows = keep.tile([PACK, 2 * P], BF16, name="floor_rows")
+        for cols, vec in ((vote_cols, vote), (intercept_cols, intercept)):
+            nc.scalar.dma_start(
+                out=cols[:].rearrange("p (g t) -> p g t", t=PACK),
+                in_=vec.rearrange("(g p t) -> p g t", p=P, t=PACK),
+            )
+        nc.scalar.dma_start(
+            out=floor_rows[:].rearrange("t (x j) -> t x j", j=4),
+            in_=floor_weight.rearrange("(x t j) -> t x j", t=PACK, j=4),
+        )
+
+        def load(key, rows):
+            raw[key] = keep.tile([P, WIDE], BF16, name="raw_%s%d%d" % key)
+            nc.sync.dma_start(
+                out=raw[key][:].rearrange("p (t c) -> p t c", t=PACK),
+                in_=rows.rearrange("(p t) c -> p t c", t=PACK),
+            )
+
+        def load_outputs(h, c):
+            key = ("out", h, c)
+            raw[key] = keep.tile([P, WIDE], BF16, name="raw_%s%d%d" % key)
+            rows = outputs[span(h), span(c)].rearrange("(a t j) u -> t a j u", t=PACK, j=4)
+            for t in range(PACK):
+                nc.sync.dma_start(out=raw[key][:, span(t)], in_=rows[t])
+
+        def load_mixes(g):
+            load(("mn", g, 0), mix_now[span(g), :])
+            for k in range(2):
+                load(("mo", g, k), mix_old[span(g), span(k)])
+
+        def load_chunk(c):
+            load(("in", 0, c), inputs[:, span(c)])
+            for h in range(2):
+                load_outputs(h, c)
+
+        old_word_rows = keep.tile([P, 4 * R], U8, name="old_word_rows")
+        def load_old_profiles():
+            nc.sync.dma_start(
+                out=old_word_rows[:].bitcast(I32).rearrange("p (k w) -> p k w", k=2),
+                in_=old_words.bitcast(I32).rearrange("k p w -> p k w"),
+            )
+            for q in range(4):
+                nc.sync.dma_start(
+                    out=old_scale_rows[32 * q : 32 * q + 4, :].bitcast(I32).rearrange("p (k w) -> p k w", k=2),
+                    in_=old_scales.bitcast(I32)[:, 4 * q : 4 * q + 4, :].rearrange("k r w -> r k w"),
+                )
+
+        def load_any(key):
+            name, a, b = key
+            if name == "out":
+                load_outputs(a, b)
+            elif name == "in":
+                load(key, inputs[:, span(b)])
+            elif name == "pn":
+                load(key, profiles_now[:, span(a)])
+            elif name == "mo":
+                load(key, mix_old[span(a), span(b)])
+            elif name == "mn":
+                load(key, mix_now[span(a), :])
+            else:
+                load(key, input_weights[span(a), :])
+
+        with tc.manual_schedule(engines={mybir.EngineType.SP}):
+            for key in LOADS:
+                if key[0] == "old":
+                    load_old_profiles()
+                else:
+                    load_any(key)
+
+        def interleave(key, src, on_scalar=0):
+            stage[key] = staged()
+            dst = stage[key][:].rearrange("p (c i t) -> p c t i", i=4, t=PACK)
+            rows = src.rearrange("p (t c i) -> p c t i", t=PACK, i=4)
+            cut = P - on_scalar
+            if cut:
+                nc.vector.tensor_copy(out=dst[:, :cut], in_=rows[:, :cut])
+            if on_scalar:
+                nc.scalar.copy(out=dst[:, cut:], in_=rows[:, cut:])
+
+        def interleave_profiles(h, on_scalar):
+            key = ("pn", h, 0)
+            stage[key] = staged()
+            dst = stage[key][:].rearrange("p (s a i t) -> p a s t i", s=PACK, i=4, t=PACK)
+            rows = raw[key][:].rearrange("p (t a s i) -> p a s t i", t=PACK, s=PACK, i=4)
+            cut = PACK - on_scalar
+            nc.vector.tensor_copy(out=dst[:, :, :cut], in_=rows[:, :, :cut])
+            if on_scalar:
+                nc.scalar.copy(out=dst[:, :, cut:], in_=rows[:, :, cut:])
+
+        def turn(key):
+            stage[key] = staged()
+            words = raw[key][:].bitcast(F32)
+            banks = [bank(), bank()]
+            for t in range(PACK):
+                for u in range(2):
+                    nc.tensor.transpose(
+                        banks[t // 2][:, part(2 * (t % 2) + u)],
+                        words[:, 256 * t + u : 256 * (t + 1) : 2],
+                        identity[:],
+                    )
+            stage[key + ("banks",)] = banks
+
+        def turn_out(key, half):
+            nc.scalar.copy(
+                out=stage[key][:].bitcast(F32)[:, span(half)].rearrange("p (s d u) -> p s d u", s=2, u=2),
+                in_=stage[key + ("banks",)][half][:].rearrange("p (s u d) -> p s d u", s=2, u=2),
+            )
+
+        def quantise(key):
+            codes = keep.tile([P, SPAN], U32, name="codes_%s%d%d" % key, align_bytes=64)
+            scales = keep.tile([P, SPAN], U8, name="scales_%s%d%d" % key, align_bytes=64)
+            nc.vector.quantize_mx(out=codes[:].bitcast(FP8X4), scales=scales[:], in_=stage[key][:])
+            packed[key] = (codes, scales)
+
+        def product(acc, passes):
+            for n, (lhs, lhs_scale, rhs_key) in enumerate(passes):
+                codes, scales = packed[rhs_key]
+                nc.tensor.matmul_mx(
+                    out=acc[:], lhsT=lhs, lhsT_scale=lhs_scale,
+                    rhs=codes[:].bitcast(FP8X4), rhs_scale=scales[:],
+                    start=(n == 0), stop=(n == len(passes) - 1),
+                )
+
+        def stationary(key, t):
+            codes, scales = packed[key]
+            return codes[:, part(t)].bitcast(FP8X4), scales[:, part(t)]
+
+        old_codes = keep.tile([P, 4 * R], U8, name="old_codes", align_bytes=64)
+        old_plane = keep.tile([P, 2 * R], U8, name="old_plane", align_bytes=64)
+
+        def sort_old_words():
+            nc.vector.tensor_copy(
+                out=old_codes[:].bitcast(I32).rearrange("p (x t a w) -> p x t a w", x=4, t=PACK, w=2),
+                in_=old_word_rows[:].bitcast(I32).rearrange("p (x a t w) -> p x t a w", x=4, t=PACK, w=2),
+            )
+
+        def sort_old_scales():
+            nc.vector.tensor_copy(
+                out=old_plane[:].bitcast(I32).rearrange("p (x t a) -> p x t a", x=4, t=PACK),
+                in_=old_scale_rows[:].bitcast(I32).rearrange("p (x a t) -> p x t a", x=4, t=PACK),
+            )
+
+        floor_cols = keep.tile([P, 2 * PACK], F32, name="floor_cols")
+        root_vote = keep.tile([P, GROUPS * PACK], F32, name="root_vote")
+        vote_scale = keep.tile([P, GROUPS * PACK], F32, name="vote_scale")
+
+        def compose(g, h, t):
+            key = ("u", g, h)
+            if t == 0:
+                raw[key] = work.tile([P, WIDE], BF16, name="u_rows", tag="u_rows")
+            acc = bank()
+            passes = [stationary(("pn", h, 0), t) + (("mn", g, 0),)]
+            for k in range(2):
+                x = (2 * k + h) * PACK + t
+                passes.append((old_codes[:, 2 * P * x : 2 * P * (x + 1)].bitcast(FP4X4), old_plane[:, part(x)], ("mo", g, k)))
+            product(acc, passes)
+            stage[key + (t,)] = acc
+
+        def compose_out(g, h, t):
+            key = ("u", g, h)
+            nc.scalar.activation(
+                out=raw[key][:, span(t)], in_=stage[key + (t,)][:], func=ACT.Identity,
+                bias=floor_cols[:, h * PACK + t : h * PACK + t + 1],
+            )
+
+        slots = [(g, c, t) for g in range(GROUPS) for c in range(CHUNKS) for t in range(PACK)]
+        y_scales = [keep.tile([P, UNITS], U8, name="y_scales%d" % g, align_bytes=64) for g in range(GROUPS)]
+
+        def weigh_inputs(s):
+            g, c, t = slots[s]
+            stage[("den", s)] = bank()
+            product(stage[("den", s)], [stationary(("iw", g, 0), t) + (("in", 0, c),)])
+
+        def weigh_outputs(s):
+            g, c, t = slots[s]
+            stage[("num", s)] = psum.tile([P, SPAN], F32, name="num", tag="num", bufs=3)
+            product(stage[("num", s)], [stationary(("u", g, h), t) + (("out", h, c),) for h in range(2)])
+
+        def inverse_root(s):
+            stage[("inv", s)] = work.tile([P, SPAN], F32, name="inv", tag="inv", bufs=AHEAD + 1)
+            nc.scalar.activation(out=stage[("inv", s)][:], in_=stage[("den", s)][:], func=ACT.Abs_reciprocal_sqrt)
+
+        def square(s):
+            g, c, t = slots[s]
+            inv = stage[("inv", s)]
+            nc.scalar.activation(out=inv[:], in_=inv[:], func=ACT.Square, scale=vote_scale[:, g * PACK + t : g * PACK + t + 1])
+
+        def score(s):
+            g, c, t = slots[s]
+            if t == 0:
+                raw[("y", g, c)] = work.tile([P, WIDE], F32, name="y_rows", tag="y_rows", bufs=2)
+            y = raw[("y", g, c)]
+            nc.vector.scalar_tensor_tensor(
+                out=y[:, span(t)], in0=stage[("num", s)][:], scalar=intercept_cols[:, g * PACK + t : g * PACK + t + 1],
+                in1=stage[("inv", s)][:], op0=ALU.add, op1=ALU.mult,
+            )
+            rows = out_0[span(g), span(c)].rearrange("(p t) u -> p t u", t=PACK)
+            nc.sync.dma_start(out=rows[:, t, :], in_=y[:, span(t)])
+
+        def quantise_scores(g, c):
+            codes = work.tile([P, SPAN], U32, name="y_codes", tag="y_codes", bufs=3, align_bytes=64)
+            nc.vector.quantize_mx(out=codes[:].bitcast(FP8X4), scales=y_scales[g][:, span(c)], in_=stage[("y", g, c)][:])
+            nc.sync.dma_start(
+                out=out_1[g].rearrange("p m t -> p (m t)").bitcast(I32)[:, span(c)], in_=codes[:].bitcast(I32)
+            )
+            if c == CHUNKS - 1:
+                for q in range(4):
+                    nc.sync.dma_start(
+                        out=out_2[g, 4 * q : 4 * q + 4, :].bitcast(I32),
+                        in_=y_scales[g][32 * q : 32 * q + 4, :].bitcast(I32),
+                    )
+
+        def il(key, n=0):
+            interleave(key, raw[key][:], n)
+
+        def den(s):
+            weigh_inputs(s)
+            inverse_root(s)
+
+        def turned(key):
+            turn(key)
+            turn_out(key, 0)
+            turn_out(key, 1)
+
+        def composed(g, h, t):
+            compose(g, h, t)
+            compose_out(g, h, t)
+
+        def floor_columns():
+            floor_bank = bank()
+            for h in range(2):
+                nc.tensor.transpose(floor_bank[:, part(h)], floor_spread[:, part(h)], identity[:])
+            nc.scalar.copy(
+                out=floor_cols[:].rearrange("p (h t) -> p h t", t=PACK),
+                in_=floor_bank[:].rearrange("p (h m) -> p h m", m=P)[:, 0:2, 0:PACK],
+            )
+
+        def weave(key, on_scalar=0):
+            if key[0] == "pn":
+                interleave_profiles(key[1], on_scalar // 32)
+            else:
+                il(key, on_scalar)
+
+        q = quantise
+        mn0, mo0, mo1, iw0 = ("mn", 0, 0), ("mo", 0, 0), ("mo", 0, 1), ("iw", 0, 0)
+        mn1, mo2, mo3, iw1 = ("mn", 1, 0), ("mo", 1, 0), ("mo", 1, 1), ("iw", 1, 0)
+        pn0, pn1 = ("pn", 0, 0), ("pn", 1, 0)
+        in0, in1, in2 = [("in", 0, c) for c in range(CHUNKS)]
+
+        nc.scalar.activation(out=root_vote[:], in_=vote_cols[:], func=ACT.Abs_reciprocal_sqrt)
+        il(("in", 0, 0), 40)
+        nc.vector.tensor_copy(out=floor_spread[0:PACK, :], in_=floor_rows[:])
+        nc.vector.tensor_tensor(out=vote_scale[:], in0=root_vote[:], in1=vote_cols[:], op=ALU.mult)
+        q(("in", 0, 0))
+        turned(iw0)
+        interleave_profiles(0, 0)
+        floor_columns()
+        turned(mn0)
+        q(iw0)
+        q(("pn", 0, 0))
+        turned(mo0)
+        q(mn0)
+        den(0)
+        den(1)
+        sort_old_words()
+        q(mo0)
+        sort_old_scales()
+        turned(mo1)
+        square(0)
+        den(2)
+        square(1)
+        den(3)
+        interleave_profiles(1, 0)
+        q(mo1)
+        square(2)
+        square(3)
+        il(("in", 0, 1))
+        q(("pn", 1, 0))
+        composed(0, 0, 0)
+        il(("out", 0, 0))
+        q(("in", 0, 1))
+        composed(0, 0, 1)
+        composed(0, 0, 2)
+        den(4)
+        composed(0, 0, 3)
+        il(("out", 1, 0))
+        q(("out", 0, 0))
+        den(5)
+        composed(0, 1, 0)
+        square(4)
+        il(("u", 0, 0))
+        q(("out", 1, 0))
+        composed(0, 1, 1)
+        square(5)
+        composed(0, 1, 2)
+        q(("u", 0, 0))
+        den(6)
+        composed(0, 1, 3)
+        den(7)
+        turned(mn1)
+        il(("out", 0, 1))
+        il(("u", 0, 1))
+        square(6)
+        square(7)
+        q(("out", 0, 1))
+        q(("u", 0, 1))
+        turned(mo2)
+        il(("out", 1, 1))
+        q(mn1)
+        turned(mo3)
+
+        extra = {
+            0: [lambda: q(("out", 1, 1)), lambda: il(("in", 0, 2))],
+            1: [lambda: q(mo2), lambda: q(("in", 0, 2)), lambda: il(("out", 0, 2), SHARE)],
+            2: [lambda: q(mo3), lambda: il(("out", 1, 2), SHARE)],
+            3: [lambda: turned(iw1), lambda: composed(1, 0, 0), lambda: q(("out", 0, 2))],
+            4: [lambda: composed(1, 0, 1), lambda: q(("out", 1, 2))],
+            5: [lambda: composed(1, 0, 2), lambda: composed(1, 0, 3), lambda: q(iw1)],
+            6: [lambda: composed(1, 1, 0), lambda: composed(1, 1, 1), lambda: il(("u", 1, 0))],
+            7: [lambda: composed(1, 1, 2), lambda: composed(1, 1, 3), lambda: q(("u", 1, 0))],
+            8: [lambda: il(("u", 1, 1))],
+            9: [lambda: q(("u", 1, 1))],
+        }
+        last = len(slots) - 1
+        weigh_outputs(0)
+        weigh_outputs(1)
+        for s in range(len(slots)):
+            g, c, t = slots[s]
+            if s + 2 <= last:
+                weigh_outputs(s + 2)
+            if 8 <= s + LEAD <= last:
+                den(s + LEAD)
+            if 8 <= s + LEAD - 1 <= last:
+                square(s + LEAD - 1)
+            score(s)
+            for step in extra.get(s, []):
+                step()
+            if t == 0 and s > 0:
+                il(("y",) + slots[s - 1][:2], YSHARE if s > 8 else 0)
+            if t == 1 and s > 1:
+                quantise_scores(*slots[s - 2][:2])
+        il(("y", GROUPS - 1, CHUNKS - 1), 40)
+        quantise_scores(GROUPS - 1, CHUNKS - 1)

@@ -23,10 +23,11 @@ WIDE = SPAN * PACK
 GROUPS = D // SPAN
 CHUNKS = UNITS // SPAN
 AHEAD = 8
-LOADS = [("in", 0, 0), ("iw", 0, 0), ("pn", 0, 0), ("mn", 0, 0), ("old", 0, 0), ("mo", 0, 0), ("pn", 1, 0), ("mo", 0, 1), ("in", 0, 1), ("out", 0, 0), ("out", 1, 0), ("out", 0, 1), ("mn", 1, 0), ("mo", 1, 0), ("mo", 1, 1), ("out", 1, 1), ("in", 0, 2), ("iw", 1, 0), ("out", 0, 2), ("out", 1, 2)]
+LOADS = [("iw", 0, 0, 1), ("in", 0, 0, 1), ("pn", 0, 0, 2), ("mn", 0, 0, 1), ("old", 0, 0, 1), ("mo", 0, 0, 2), ("in", 0, 1, 1), ("out", 0, 0, 3), ("mn", 1, 0, 1), ("out", 1, 0, 3), ("mo", 1, 0, 2), ("in", 0, 2, 1), ("iw", 1, 0, 1)]
 SHARE = 64
-YSHARE = 32
+YSHARE = 48
 LEAD = 4
+HEAD = 32
 
 
 def tile_cross_efficiency_composed_weights_k6_kernel(
@@ -51,53 +52,36 @@ def tile_cross_efficiency_composed_weights_k6_kernel(
         def staged():
             return work.tile([P, WIDE], BF16, name="staged", tag="staged", bufs=6, align_bytes=64)
 
-        raw, packed, stage = {}, {}, {}
+        raw, words, packed, stage = {}, {}, {}, {}
 
         identity = keep.tile([P, P], F32, name="identity")
         make_identity(nc, identity[:])
         old_scale_rows = keep.tile([P, 2 * R], U8, name="old_scale_rows")
         nc.gpsimd.memset(old_scale_rows[:].bitcast(I32), 0)
-        floor_spread = keep.tile([P, 2 * P], F32, name="floor_spread")
-        nc.gpsimd.memset(floor_spread[:], 0.0)
+        spread = keep.tile([P, SPAN], F32, name="spread")
+        nc.gpsimd.memset(spread[:], 0.0)
 
-        vote_cols = keep.tile([P, GROUPS * PACK], BF16, name="vote_cols")
-        intercept_cols = keep.tile([P, GROUPS * PACK], BF16, name="intercept_cols")
-        floor_rows = keep.tile([PACK, 2 * P], BF16, name="floor_rows")
-        for cols, vec in ((vote_cols, vote), (intercept_cols, intercept)):
-            nc.scalar.dma_start(
-                out=cols[:].rearrange("p (g t) -> p g t", t=PACK),
-                in_=vec.rearrange("(g p t) -> p g t", p=P, t=PACK),
-            )
-        nc.scalar.dma_start(
-            out=floor_rows[:].rearrange("t (x j) -> t x j", j=4),
-            in_=floor_weight.rearrange("(x t j) -> t x j", t=PACK, j=4),
-        )
+        vectors = keep.tile([P, SPAN], BF16, name="vectors")
+        with tc.manual_schedule(engines={mybir.EngineType.Activation}):
+            for n, vec in enumerate((vote, intercept, floor_weight)):
+                nc.scalar.dma_start(out=vectors[32 * n : 32 * n + 2, :], in_=vec.rearrange("(g c) -> g c", g=2))
 
-        def load(key, rows):
-            raw[key] = keep.tile([P, WIDE], BF16, name="raw_%s%d%d" % key)
-            nc.sync.dma_start(
-                out=raw[key][:].rearrange("p (t c) -> p t c", t=PACK),
-                in_=rows.rearrange("(p t) c -> p t c", t=PACK),
-            )
-
-        def load_outputs(h, c):
-            key = ("out", h, c)
-            raw[key] = keep.tile([P, WIDE], BF16, name="raw_%s%d%d" % key)
-            rows = outputs[span(h), span(c)].rearrange("(a t j) u -> t a j u", t=PACK, j=4)
-            for t in range(PACK):
-                nc.sync.dma_start(out=raw[key][:, span(t)], in_=rows[t])
-
-        def load_mixes(g):
-            load(("mn", g, 0), mix_now[span(g), :])
-            for k in range(2):
-                load(("mo", g, k), mix_old[span(g), span(k)])
-
-        def load_chunk(c):
-            load(("in", 0, c), inputs[:, span(c)])
-            for h in range(2):
-                load_outputs(h, c)
+        def load(name, first, count, rows):
+            loaded = keep.tile([P, PACK * count * SPAN], BF16, name="raw_%s%d%d" % (name, first[0], first[1]))
+            view = loaded[:].rearrange("p (t c) -> p t c", t=PACK)
+            if name == "out":
+                runs = rows.rearrange("(a t j) u -> t a j u", t=PACK, j=4)
+                for t in range(PACK):
+                    nc.sync.dma_start(out=view[:, t, :], in_=runs[t])
+            else:
+                nc.sync.dma_start(out=view, in_=rows.rearrange("(p t) c -> p t c", t=PACK))
+            for n in range(count):
+                key = (name, first[0] + n, 0) if name == "pn" else (name, first[0], first[1] + n)
+                raw[key] = view[:, :, span(n)]
+                words[key] = (loaded[:].bitcast(F32), count * SPAN // 2, n * SPAN // 2)
 
         old_word_rows = keep.tile([P, 4 * R], U8, name="old_word_rows")
+
         def load_old_profiles():
             nc.sync.dma_start(
                 out=old_word_rows[:].bitcast(I32).rearrange("p (k w) -> p k w", k=2),
@@ -109,32 +93,31 @@ def tile_cross_efficiency_composed_weights_k6_kernel(
                     in_=old_scales.bitcast(I32)[:, 4 * q : 4 * q + 4, :].rearrange("k r w -> r k w"),
                 )
 
-        def load_any(key):
-            name, a, b = key
-            if name == "out":
-                load_outputs(a, b)
+        def load_any(name, a, b, count):
+            cols = slice(b * SPAN, (b + count) * SPAN)
+            if name == "old":
+                load_old_profiles()
+            elif name == "out":
+                load(name, (a, b), count, outputs[span(a), cols])
             elif name == "in":
-                load(key, inputs[:, span(b)])
+                load(name, (a, b), count, inputs[:, cols])
             elif name == "pn":
-                load(key, profiles_now[:, span(a)])
+                load(name, (a, b), count, profiles_now[:, a * SPAN : (a + count) * SPAN])
             elif name == "mo":
-                load(key, mix_old[span(a), span(b)])
+                load(name, (a, b), count, mix_old[span(a), cols])
             elif name == "mn":
-                load(key, mix_now[span(a), :])
+                load(name, (a, b), count, mix_now[span(a), :])
             else:
-                load(key, input_weights[span(a), :])
+                load(name, (a, b), count, input_weights[span(a), :])
 
         with tc.manual_schedule(engines={mybir.EngineType.SP}):
-            for key in LOADS:
-                if key[0] == "old":
-                    load_old_profiles()
-                else:
-                    load_any(key)
+            for entry in LOADS:
+                load_any(*entry)
 
         def interleave(key, src, on_scalar=0):
             stage[key] = staged()
             dst = stage[key][:].rearrange("p (c i t) -> p c t i", i=4, t=PACK)
-            rows = src.rearrange("p (t c i) -> p c t i", t=PACK, i=4)
+            rows = src.rearrange("p t (c i) -> p c t i", i=4)
             cut = P - on_scalar
             if cut:
                 nc.vector.tensor_copy(out=dst[:, :cut], in_=rows[:, :cut])
@@ -145,7 +128,7 @@ def tile_cross_efficiency_composed_weights_k6_kernel(
             key = ("pn", h, 0)
             stage[key] = staged()
             dst = stage[key][:].rearrange("p (s a i t) -> p a s t i", s=PACK, i=4, t=PACK)
-            rows = raw[key][:].rearrange("p (t a s i) -> p a s t i", t=PACK, s=PACK, i=4)
+            rows = raw[key].rearrange("p t (a s i) -> p a s t i", s=PACK, i=4)
             cut = PACK - on_scalar
             nc.vector.tensor_copy(out=dst[:, :, :cut], in_=rows[:, :, :cut])
             if on_scalar:
@@ -153,13 +136,13 @@ def tile_cross_efficiency_composed_weights_k6_kernel(
 
         def turn(key):
             stage[key] = staged()
-            words = raw[key][:].bitcast(F32)
+            pairs, pitch, first = words[key]
             banks = [bank(), bank()]
             for t in range(PACK):
                 for u in range(2):
                     nc.tensor.transpose(
                         banks[t // 2][:, part(2 * (t % 2) + u)],
-                        words[:, 256 * t + u : 256 * (t + 1) : 2],
+                        pairs[:, pitch * t + first + u : pitch * t + first + 2 * P : 2],
                         identity[:],
                     )
             stage[key + ("banks",)] = banks
@@ -204,14 +187,34 @@ def tile_cross_efficiency_composed_weights_k6_kernel(
                 in_=old_scale_rows[:].bitcast(I32).rearrange("p (x a t) -> p x t a", x=4, t=PACK),
             )
 
-        floor_cols = keep.tile([P, 2 * PACK], F32, name="floor_cols")
-        root_vote = keep.tile([P, GROUPS * PACK], F32, name="root_vote")
-        vote_scale = keep.tile([P, GROUPS * PACK], F32, name="vote_scale")
+        columns = keep.tile([P, PACK, 3, 2], F32, name="columns")
+
+        def column(n, g, t):
+            return columns[:, t, n, g : g + 1]
+
+        def sort_vectors():
+            by_slot = vectors[:].rearrange("p (c t) -> p t c", t=PACK)
+            by_run = vectors[:].rearrange("p (a t j) -> p t a j", t=PACK, j=4)
+            slots_out = spread[:].rearrange("p (t c) -> p t c", t=PACK)
+            runs_out = spread[:].rearrange("p (t a j) -> p t a j", t=PACK, j=4)
+            nc.scalar.activation(out=slots_out[0:2], in_=by_slot[0:2], func=ACT.Abs_reciprocal_sqrt)
+            nc.scalar.copy(out=slots_out[32:34], in_=by_slot[32:34])
+            nc.scalar.copy(out=runs_out[64:66], in_=by_run[64:66])
+            nc.vector.tensor_tensor(out=slots_out[0:2], in0=slots_out[0:2], in1=by_slot[0:2], op=ALU.mult)
+
+        def turn_vectors():
+            turned_bank = bank()
+            for t in range(PACK):
+                nc.tensor.transpose(turned_bank[:, part(t)], spread[:, part(t)], identity[:])
+            nc.scalar.copy(
+                out=columns[:],
+                in_=turned_bank[:].rearrange("p (t n r) -> p t n r", t=PACK, r=32)[:, :, 0:3, 0:2],
+            )
 
         def compose(g, h, t):
             key = ("u", g, h)
             if t == 0:
-                raw[key] = work.tile([P, WIDE], BF16, name="u_rows", tag="u_rows")
+                raw[key] = work.tile([P, PACK, SPAN], BF16, name="u_rows", tag="u_rows")[:]
             acc = bank()
             passes = [stationary(("pn", h, 0), t) + (("mn", g, 0),)]
             for k in range(2):
@@ -223,8 +226,8 @@ def tile_cross_efficiency_composed_weights_k6_kernel(
         def compose_out(g, h, t):
             key = ("u", g, h)
             nc.scalar.activation(
-                out=raw[key][:, span(t)], in_=stage[key + (t,)][:], func=ACT.Identity,
-                bias=floor_cols[:, h * PACK + t : h * PACK + t + 1],
+                out=raw[key][:, t, :], in_=stage[key + (t,)][:], func=ACT.Identity,
+                bias=column(2, h, t),
             )
 
         slots = [(g, c, t) for g in range(GROUPS) for c in range(CHUNKS) for t in range(PACK)]
@@ -247,19 +250,19 @@ def tile_cross_efficiency_composed_weights_k6_kernel(
         def square(s):
             g, c, t = slots[s]
             inv = stage[("inv", s)]
-            nc.scalar.activation(out=inv[:], in_=inv[:], func=ACT.Square, scale=vote_scale[:, g * PACK + t : g * PACK + t + 1])
+            nc.scalar.activation(out=inv[:], in_=inv[:], func=ACT.Square, scale=column(0, g, t))
 
         def score(s):
             g, c, t = slots[s]
             if t == 0:
-                raw[("y", g, c)] = work.tile([P, WIDE], F32, name="y_rows", tag="y_rows", bufs=2)
+                raw[("y", g, c)] = work.tile([P, PACK, SPAN], F32, name="y_rows", tag="y_rows", bufs=3)[:]
             y = raw[("y", g, c)]
             nc.vector.scalar_tensor_tensor(
-                out=y[:, span(t)], in0=stage[("num", s)][:], scalar=intercept_cols[:, g * PACK + t : g * PACK + t + 1],
+                out=y[:, t, :], in0=stage[("num", s)][:], scalar=column(1, g, t),
                 in1=stage[("inv", s)][:], op0=ALU.add, op1=ALU.mult,
             )
             rows = out_0[span(g), span(c)].rearrange("(p t) u -> p t u", t=PACK)
-            nc.sync.dma_start(out=rows[:, t, :], in_=y[:, span(t)])
+            nc.sync.dma_start(out=rows[:, t, :], in_=y[:, t, :])
 
         def quantise_scores(g, c):
             codes = work.tile([P, SPAN], U32, name="y_codes", tag="y_codes", bufs=3, align_bytes=64)
@@ -275,7 +278,7 @@ def tile_cross_efficiency_composed_weights_k6_kernel(
                     )
 
         def il(key, n=0):
-            interleave(key, raw[key][:], n)
+            interleave(key, raw[key], n)
 
         def den(s):
             weigh_inputs(s)
@@ -290,15 +293,6 @@ def tile_cross_efficiency_composed_weights_k6_kernel(
             compose(g, h, t)
             compose_out(g, h, t)
 
-        def floor_columns():
-            floor_bank = bank()
-            for h in range(2):
-                nc.tensor.transpose(floor_bank[:, part(h)], floor_spread[:, part(h)], identity[:])
-            nc.scalar.copy(
-                out=floor_cols[:].rearrange("p (h t) -> p h t", t=PACK),
-                in_=floor_bank[:].rearrange("p (h m) -> p h m", m=P)[:, 0:2, 0:PACK],
-            )
-
         def weave(key, on_scalar=0):
             if key[0] == "pn":
                 interleave_profiles(key[1], on_scalar // 32)
@@ -311,29 +305,27 @@ def tile_cross_efficiency_composed_weights_k6_kernel(
         pn0, pn1 = ("pn", 0, 0), ("pn", 1, 0)
         in0, in1, in2 = [("in", 0, c) for c in range(CHUNKS)]
 
-        nc.scalar.activation(out=root_vote[:], in_=vote_cols[:], func=ACT.Abs_reciprocal_sqrt)
-        il(("in", 0, 0), 40)
-        nc.vector.tensor_copy(out=floor_spread[0:PACK, :], in_=floor_rows[:])
-        nc.vector.tensor_tensor(out=vote_scale[:], in0=root_vote[:], in1=vote_cols[:], op=ALU.mult)
-        q(("in", 0, 0))
+        sort_vectors()
         turned(iw0)
-        interleave_profiles(0, 0)
-        floor_columns()
-        turned(mn0)
+        il(("in", 0, 0), HEAD)
+        turn_vectors()
+        q(("in", 0, 0))
         q(iw0)
-        q(("pn", 0, 0))
-        turned(mo0)
-        q(mn0)
         den(0)
         den(1)
-        sort_old_words()
-        q(mo0)
-        sort_old_scales()
-        turned(mo1)
+        interleave_profiles(0, 0)
         square(0)
         den(2)
         square(1)
         den(3)
+        turned(mn0)
+        q(("pn", 0, 0))
+        q(mn0)
+        sort_old_words()
+        sort_old_scales()
+        turned(mo0)
+        q(mo0)
+        turned(mo1)
         interleave_profiles(1, 0)
         q(mo1)
         square(2)

@@ -17,17 +17,26 @@ ACT = mybir.ActivationFunctionType
 ALU = mybir.AluOpType
 
 P = 128
-PACK = 4
-SPAN = P * PACK
-WIDE = SPAN * PACK
+SLOTS = 4
+RUN = 4
+SPAN = P * SLOTS
+WIDE = SPAN * SLOTS
 GROUPS = D // SPAN
+HALVES = R // SPAN
 CHUNKS = UNITS // SPAN
-AHEAD = 8
-LOADS = [("iw", 0, 0, 1), ("in", 0, 0, 1), ("pn", 0, 0, 2), ("mn", 0, 0, 1), ("old", 0, 0, 1), ("mo", 0, 0, 2), ("in", 0, 1, 1), ("out", 0, 0, 3), ("mn", 1, 0, 1), ("out", 1, 0, 3), ("mo", 1, 0, 2), ("in", 0, 2, 1), ("iw", 1, 0, 1)]
-SHARE = 64
-YSHARE = 48
-LEAD = 4
-HEAD = 32
+VOTE, INTERCEPT, FLOOR = 0, 1, 2
+
+LOADS = [
+    ("input_weights", 0, 0, 1), ("inputs", 0, 0, 1), ("profiles_now", 0, 0, 2), ("mix_now", 0, 0, 1),
+    ("inputs", 0, 1, 2), ("profiles_old", 0, 0, 1), ("mix_old", 0, 0, 2), ("outputs", 0, 0, 3),
+    ("mix_now", 1, 0, 1), ("mix_old", 1, 0, 2), ("outputs", 1, 0, 3), ("input_weights", 1, 0, 1),
+]
+EARLY_LOADS = 8
+
+LEAD = 10
+DIVISOR_TILES = 13
+GPSIMD_RUNS = 72
+LAST_SCALAR_RUNS = 40
 
 
 def tile_cross_efficiency_composed_weights_k6_kernel(
@@ -38,7 +47,8 @@ def tile_cross_efficiency_composed_weights_k6_kernel(
     with ExitStack() as ctx:
         keep = ctx.enter_context(tc.tile_pool(name="keep", bufs=1))
         work = ctx.enter_context(tc.tile_pool(name="work", bufs=2))
-        psum = ctx.enter_context(tc.psum_pool(name="psum", bufs=8))
+        psum = ctx.enter_context(tc.psum_pool(name="psum", bufs=4))
+        ctx.enter_context(tc.manual_schedule())
 
         def span(i):
             return slice(i * SPAN, (i + 1) * SPAN)
@@ -47,226 +57,243 @@ def tile_cross_efficiency_composed_weights_k6_kernel(
             return slice(i * P, (i + 1) * P)
 
         def bank():
-            return psum.tile([P, SPAN], F32, name="bank", tag="bank", bufs=5)
+            return psum.tile([P, SPAN], F32, name="bank", tag="bank")
 
-        def staged():
-            return work.tile([P, WIDE], BF16, name="staged", tag="staged", bufs=6, align_bytes=64)
+        def numerator_bank():
+            return psum.tile([P, SPAN], F32, name="numerator", tag="numerator")
 
-        raw, words, packed, stage = {}, {}, {}, {}
+        rows_of = {}
+        words_of = {}
+        staged = {}
+        packed = {}
+        banks = {}
+        divisors = {}
+
+        def staging_tile():
+            return work.tile([P, WIDE], BF16, name="staged", tag="staged", bufs=5, align_bytes=64)
+
+        def shared_staging_tile():
+            return work.tile([P, WIDE], BF16, name="shared", tag="shared", bufs=1, align_bytes=64)
 
         identity = keep.tile([P, P], F32, name="identity")
         make_identity(nc, identity[:])
-        old_scale_rows = keep.tile([P, 2 * R], U8, name="old_scale_rows")
+        old_scale_rows = keep.tile([P, HALVES * R], U8, name="old_scale_rows")
         nc.gpsimd.memset(old_scale_rows[:].bitcast(I32), 0)
-        spread = keep.tile([P, SPAN], F32, name="spread")
-        nc.gpsimd.memset(spread[:], 0.0)
+        sorted_vectors = keep.tile([P, SPAN], F32, name="sorted_vectors")
+        nc.gpsimd.memset(sorted_vectors[:], 0.0)
 
         vectors = keep.tile([P, SPAN], BF16, name="vectors")
-        with tc.manual_schedule(engines={mybir.EngineType.Activation}):
-            for n, vec in enumerate((vote, intercept, floor_weight)):
-                nc.scalar.dma_start(out=vectors[32 * n : 32 * n + 2, :], in_=vec.rearrange("(g c) -> g c", g=2))
+        for n, vector in ((VOTE, vote), (INTERCEPT, intercept), (FLOOR, floor_weight)):
+            nc.sync.dma_start(out=vectors[32 * n : 32 * n + 2, :], in_=vector.rearrange("(g c) -> g c", g=2))
 
-        def load(name, first, count, rows):
-            loaded = keep.tile([P, PACK * count * SPAN], BF16, name="raw_%s%d%d" % (name, first[0], first[1]))
-            view = loaded[:].rearrange("p (t c) -> p t c", t=PACK)
-            if name == "out":
-                runs = rows.rearrange("(a t j) u -> t a j u", t=PACK, j=4)
-                for t in range(PACK):
-                    nc.sync.dma_start(out=view[:, t, :], in_=runs[t])
-            else:
-                nc.sync.dma_start(out=view, in_=rows.rearrange("(p t) c -> p t c", t=PACK))
-            for n in range(count):
-                key = (name, first[0] + n, 0) if name == "pn" else (name, first[0], first[1] + n)
-                raw[key] = view[:, :, span(n)]
-                words[key] = (loaded[:].bitcast(F32), count * SPAN // 2, n * SPAN // 2)
-
-        old_word_rows = keep.tile([P, 4 * R], U8, name="old_word_rows")
+        old_word_rows = keep.tile([P, HALVES * 2 * R], U8, name="old_word_rows")
 
         def load_old_profiles():
             nc.sync.dma_start(
-                out=old_word_rows[:].bitcast(I32).rearrange("p (k w) -> p k w", k=2),
+                out=old_word_rows[:].bitcast(I32).rearrange("p (k w) -> p k w", k=HALVES),
                 in_=old_words.bitcast(I32).rearrange("k p w -> p k w"),
             )
             for q in range(4):
                 nc.sync.dma_start(
-                    out=old_scale_rows[32 * q : 32 * q + 4, :].bitcast(I32).rearrange("p (k w) -> p k w", k=2),
+                    out=old_scale_rows[32 * q : 32 * q + 4, :].bitcast(I32).rearrange("p (k w) -> p k w", k=HALVES),
                     in_=old_scales.bitcast(I32)[:, 4 * q : 4 * q + 4, :].rearrange("k r w -> r k w"),
                 )
 
-        def load_any(name, a, b, count):
-            cols = slice(b * SPAN, (b + count) * SPAN)
-            if name == "old":
+        row_blocks = {"mix_now": mix_now, "mix_old": mix_old, "input_weights": input_weights, "inputs": inputs,
+                      "profiles_now": profiles_now, "outputs": outputs}
+
+        def load(operand, i, j, count):
+            if operand == "profiles_old":
                 load_old_profiles()
-            elif name == "out":
-                load(name, (a, b), count, outputs[span(a), cols])
-            elif name == "in":
-                load(name, (a, b), count, inputs[:, cols])
-            elif name == "pn":
-                load(name, (a, b), count, profiles_now[:, a * SPAN : (a + count) * SPAN])
-            elif name == "mo":
-                load(name, (a, b), count, mix_old[span(a), cols])
-            elif name == "mn":
-                load(name, (a, b), count, mix_now[span(a), :])
+                return
+            rows = row_blocks[operand][span(i), j * SPAN : (j + count) * SPAN]
+            label = "load_%s_%d_%d" % (operand, i, j)
+            tag = "load_" + operand if operand in ("mix_now", "input_weights") else label
+            loaded = keep.tile([P, count * WIDE], BF16, name=label, tag=tag)
+            view = loaded[:].rearrange("p (t c) -> p t c", t=SLOTS)
+            if operand == "outputs":
+                runs = rows.rearrange("(a t j) u -> t a j u", t=SLOTS, j=4)
+                for t in range(SLOTS):
+                    nc.sync.dma_start(out=view[:, t, :], in_=runs[t])
             else:
-                load(name, (a, b), count, input_weights[span(a), :])
+                nc.sync.dma_start(out=view, in_=rows.rearrange("(p t) c -> p t c", t=SLOTS))
+            for n in range(count):
+                rows_of[(operand, i, j + n)] = view[:, :, span(n)]
+                words_of[(operand, i, j + n)] = (loaded[:].bitcast(F32), count * SPAN // 2, n * SPAN // 2)
 
-        with tc.manual_schedule(engines={mybir.EngineType.SP}):
-            for entry in LOADS:
-                load_any(*entry)
+        for entry in LOADS[:EARLY_LOADS]:
+            load(*entry)
 
-        def interleave(key, src, on_scalar=0):
-            stage[key] = staged()
-            dst = stage[key][:].rearrange("p (c i t) -> p c t i", i=4, t=PACK)
-            rows = src.rearrange("p t (c i) -> p c t i", i=4)
-            cut = P - on_scalar
-            if cut:
-                nc.vector.tensor_copy(out=dst[:, :cut], in_=rows[:, :cut])
-            if on_scalar:
-                nc.scalar.copy(out=dst[:, cut:], in_=rows[:, cut:])
+        def interleave_runs(piece, first, count, engine):
+            if engine == "gpsimd":
+                taken = slice(RUN * first, RUN * (first + count))
+                nc.gpsimd.tensor_scalar(
+                    out=staged[piece][:].rearrange("p (w t) -> p w t", t=SLOTS)[:, taken],
+                    in0=rows_of[piece].rearrange("p t w -> p w t")[:, taken],
+                    scalar1=1.0, scalar2=0.0, op0=ALU.mult, op1=ALU.add,
+                )
+                return
+            dst = staged[piece][:].rearrange("p (c i t) -> p c t i", i=RUN, t=SLOTS)[:, first : first + count]
+            src = rows_of[piece].rearrange("p t (c i) -> p c t i", i=RUN)[:, first : first + count]
+            if engine == "scalar":
+                nc.scalar.copy(out=dst, in_=src)
+            else:
+                nc.vector.tensor_copy(out=dst, in_=src)
 
-        def interleave_profiles(h, on_scalar):
-            key = ("pn", h, 0)
-            stage[key] = staged()
-            dst = stage[key][:].rearrange("p (s a i t) -> p a s t i", s=PACK, i=4, t=PACK)
-            rows = raw[key].rearrange("p t (a s i) -> p a s t i", s=PACK, i=4)
-            cut = PACK - on_scalar
-            nc.vector.tensor_copy(out=dst[:, :, :cut], in_=rows[:, :, :cut])
-            if on_scalar:
-                nc.scalar.copy(out=dst[:, :, cut:], in_=rows[:, :, cut:])
+        def interleave(piece):
+            staged[piece] = staging_tile()
+            interleave_runs(piece, 0, P, "vector")
 
-        def turn(key):
-            stage[key] = staged()
-            pairs, pitch, first = words[key]
-            banks = [bank(), bank()]
-            for t in range(PACK):
+        def interleave_profiles(h, vector_slots):
+            piece = ("profiles_now", 0, h)
+            staged[piece] = staging_tile()
+            dst = staged[piece][:].rearrange("p (s a i t) -> p a s t i", s=SLOTS, i=4, t=SLOTS)
+            src = rows_of[piece].rearrange("p t (a s i) -> p a s t i", s=SLOTS, i=4)
+            nc.vector.tensor_copy(out=dst[:, :, :vector_slots], in_=src[:, :, :vector_slots])
+            if vector_slots < SLOTS:
+                nc.scalar.copy(out=dst[:, :, vector_slots:], in_=src[:, :, vector_slots:])
+
+        def turn(piece):
+            staged[piece] = staging_tile()
+            pairs, pitch, first = words_of[piece]
+            turned = [bank(), bank()]
+            for t in range(SLOTS):
                 for u in range(2):
+                    start = pitch * t + first
                     nc.tensor.transpose(
-                        banks[t // 2][:, part(2 * (t % 2) + u)],
-                        pairs[:, pitch * t + first + u : pitch * t + first + 2 * P : 2],
-                        identity[:],
+                        turned[t // 2][:, part(2 * (t % 2) + u)], pairs[:, start + u : start + 2 * P : 2], identity[:]
                     )
-            stage[key + ("banks",)] = banks
-
-        def turn_out(key, half):
-            nc.scalar.copy(
-                out=stage[key][:].bitcast(F32)[:, span(half)].rearrange("p (s d u) -> p s d u", s=2, u=2),
-                in_=stage[key + ("banks",)][half][:].rearrange("p (s u d) -> p s d u", s=2, u=2),
-            )
-
-        def quantise(key):
-            codes = keep.tile([P, SPAN], U32, name="codes_%s%d%d" % key, align_bytes=64)
-            scales = keep.tile([P, SPAN], U8, name="scales_%s%d%d" % key, align_bytes=64)
-            nc.vector.quantize_mx(out=codes[:].bitcast(FP8X4), scales=scales[:], in_=stage[key][:])
-            packed[key] = (codes, scales)
-
-        def product(acc, passes):
-            for n, (lhs, lhs_scale, rhs_key) in enumerate(passes):
-                codes, scales = packed[rhs_key]
-                nc.tensor.matmul_mx(
-                    out=acc[:], lhsT=lhs, lhsT_scale=lhs_scale,
-                    rhs=codes[:].bitcast(FP8X4), rhs_scale=scales[:],
-                    start=(n == 0), stop=(n == len(passes) - 1),
+            for n in range(2):
+                nc.scalar.copy(
+                    out=staged[piece][:].bitcast(F32)[:, span(n)].rearrange("p (s d u) -> p s d u", s=2, u=2),
+                    in_=turned[n][:].rearrange("p (s u d) -> p s d u", s=2, u=2),
                 )
 
-        def stationary(key, t):
-            codes, scales = packed[key]
-            return codes[:, part(t)].bitcast(FP8X4), scales[:, part(t)]
+        def quantise(piece):
+            codes = keep.tile([P, SPAN], U32, name="codes_%s_%d_%d" % piece, align_bytes=64)
+            scales = keep.tile([P, SPAN], U8, name="scales_%s_%d_%d" % piece, align_bytes=64)
+            nc.vector.quantize_mx(out=codes[:].bitcast(FP8X4), scales=scales[:], in_=staged[piece][:])
+            packed[piece] = (codes, scales)
 
-        old_codes = keep.tile([P, 4 * R], U8, name="old_codes", align_bytes=64)
-        old_plane = keep.tile([P, 2 * R], U8, name="old_plane", align_bytes=64)
+        old_codes = keep.tile([P, HALVES * 2 * R], U8, name="old_codes", align_bytes=64)
+        old_plane = keep.tile([P, HALVES * R], U8, name="old_plane", align_bytes=64)
 
         def sort_old_words():
             nc.vector.tensor_copy(
-                out=old_codes[:].bitcast(I32).rearrange("p (x t a w) -> p x t a w", x=4, t=PACK, w=2),
-                in_=old_word_rows[:].bitcast(I32).rearrange("p (x a t w) -> p x t a w", x=4, t=PACK, w=2),
+                out=old_codes[:].bitcast(I32).rearrange("p (x s a w) -> p x s a w", x=4, s=SLOTS, w=2),
+                in_=old_word_rows[:].bitcast(I32).rearrange("p (x a s w) -> p x s a w", x=4, s=SLOTS, w=2),
             )
 
         def sort_old_scales():
             nc.vector.tensor_copy(
-                out=old_plane[:].bitcast(I32).rearrange("p (x t a) -> p x t a", x=4, t=PACK),
-                in_=old_scale_rows[:].bitcast(I32).rearrange("p (x a t) -> p x t a", x=4, t=PACK),
+                out=old_plane[:].bitcast(I32).rearrange("p (x s a) -> p x s a", x=4, s=SLOTS),
+                in_=old_scale_rows[:].bitcast(I32).rearrange("p (x a s) -> p x s a", x=4, s=SLOTS),
             )
 
-        columns = keep.tile([P, PACK, 3, 2], F32, name="columns")
+        columns = keep.tile([P, SLOTS, 3, 2], F32, name="columns")
 
         def column(n, g, t):
             return columns[:, t, n, g : g + 1]
 
         def sort_vectors():
-            by_slot = vectors[:].rearrange("p (c t) -> p t c", t=PACK)
-            by_run = vectors[:].rearrange("p (a t j) -> p t a j", t=PACK, j=4)
-            slots_out = spread[:].rearrange("p (t c) -> p t c", t=PACK)
-            runs_out = spread[:].rearrange("p (t a j) -> p t a j", t=PACK, j=4)
-            nc.scalar.activation(out=slots_out[0:2], in_=by_slot[0:2], func=ACT.Abs_reciprocal_sqrt)
-            nc.scalar.copy(out=slots_out[32:34], in_=by_slot[32:34])
-            nc.scalar.copy(out=runs_out[64:66], in_=by_run[64:66])
-            nc.vector.tensor_tensor(out=slots_out[0:2], in0=slots_out[0:2], in1=by_slot[0:2], op=ALU.mult)
+            by_slot = vectors[:].rearrange("p (c t) -> p t c", t=SLOTS)
+            by_run = vectors[:].rearrange("p (a t j) -> p t a j", t=SLOTS, j=4)
+            slot_rows = sorted_vectors[:].rearrange("p (t c) -> p t c", t=SLOTS)
+            run_rows = sorted_vectors[:].rearrange("p (t a j) -> p t a j", t=SLOTS, j=4)
+            votes, intercepts, floors = [slice(32 * n, 32 * n + 2) for n in (VOTE, INTERCEPT, FLOOR)]
+            nc.scalar.activation(out=slot_rows[votes], in_=by_slot[votes], func=ACT.Abs_reciprocal_sqrt)
+            nc.scalar.copy(out=slot_rows[intercepts], in_=by_slot[intercepts])
+            nc.scalar.copy(out=run_rows[floors], in_=by_run[floors])
+            nc.vector.tensor_tensor(out=slot_rows[votes], in0=slot_rows[votes], in1=by_slot[votes], op=ALU.mult)
 
         def turn_vectors():
-            turned_bank = bank()
-            for t in range(PACK):
-                nc.tensor.transpose(turned_bank[:, part(t)], spread[:, part(t)], identity[:])
+            turned = bank()
+            for t in range(SLOTS):
+                nc.tensor.transpose(turned[:, part(t)], sorted_vectors[:, part(t)], identity[:])
             nc.scalar.copy(
-                out=columns[:],
-                in_=turned_bank[:].rearrange("p (t n r) -> p t n r", t=PACK, r=32)[:, :, 0:3, 0:2],
+                out=columns[:], in_=turned[:].rearrange("p (t n r) -> p t n r", t=SLOTS, r=32)[:, :, 0:3, 0:2]
+            )
+
+        def stationary(piece, t):
+            codes, scales = packed[piece]
+            return codes[:, part(t)].bitcast(FP8X4), scales[:, part(t)]
+
+        def mx_pass(acc, lhs, moving_piece, start, stop):
+            codes, scales = packed[moving_piece]
+            nc.tensor.matmul_mx(
+                out=acc[:], lhsT=lhs[0], lhsT_scale=lhs[1],
+                rhs=codes[:].bitcast(FP8X4), rhs_scale=scales[:], start=start, stop=stop,
+            )
+
+        def compose_now(g, h, t, new_bank):
+            if t == 0:
+                rows_of[("U", g, h)] = work.tile([P, SLOTS, SPAN], BF16, name="u_rows", tag="u_rows")[:]
+            banks[("U", g, h, t)] = new_bank()
+            mx_pass(banks[("U", g, h, t)], stationary(("profiles_now", 0, h), t), ("mix_now", g, 0), True, False)
+
+        def compose_old(g, h, t, k):
+            x = (HALVES * k + h) * SLOTS + t
+            lhs = (old_codes[:, 2 * P * x : 2 * P * (x + 1)].bitcast(FP4X4), old_plane[:, part(x)])
+            mx_pass(banks[("U", g, h, t)], lhs, ("mix_old", g, k), False, k == HALVES - 1)
+
+        def add_floor(g, h, t):
+            nc.scalar.activation(
+                out=rows_of[("U", g, h)][:, t, :], in_=banks[("U", g, h, t)][:],
+                func=ACT.Identity, bias=column(FLOOR, h, t),
             )
 
         def compose(g, h, t):
-            key = ("u", g, h)
-            if t == 0:
-                raw[key] = work.tile([P, PACK, SPAN], BF16, name="u_rows", tag="u_rows")[:]
-            acc = bank()
-            passes = [stationary(("pn", h, 0), t) + (("mn", g, 0),)]
-            for k in range(2):
-                x = (2 * k + h) * PACK + t
-                passes.append((old_codes[:, 2 * P * x : 2 * P * (x + 1)].bitcast(FP4X4), old_plane[:, part(x)], ("mo", g, k)))
-            product(acc, passes)
-            stage[key + (t,)] = acc
+            compose_now(g, h, t, bank)
+            for k in range(HALVES):
+                compose_old(g, h, t, k)
+            add_floor(g, h, t)
 
-        def compose_out(g, h, t):
-            key = ("u", g, h)
-            nc.scalar.activation(
-                out=raw[key][:, t, :], in_=stage[key + (t,)][:], func=ACT.Identity,
-                bias=column(2, h, t),
-            )
-
-        slots = [(g, c, t) for g in range(GROUPS) for c in range(CHUNKS) for t in range(PACK)]
+        scores = [(g, c, t) for g in range(GROUPS) for c in range(CHUNKS) for t in range(SLOTS)]
+        rounds = len(scores) // SLOTS
         y_scales = [keep.tile([P, UNITS], U8, name="y_scales%d" % g, align_bytes=64) for g in range(GROUPS)]
 
-        def weigh_inputs(s):
-            g, c, t = slots[s]
-            stage[("den", s)] = bank()
-            product(stage[("den", s)], [stationary(("iw", g, 0), t) + (("in", 0, c),)])
-
-        def weigh_outputs(s):
-            g, c, t = slots[s]
-            stage[("num", s)] = psum.tile([P, SPAN], F32, name="num", tag="num", bufs=3)
-            product(stage[("num", s)], [stationary(("u", g, h), t) + (("out", h, c),) for h in range(2)])
+        def banks_of(j):
+            return range(SLOTS * j, SLOTS * (j + 1))
 
         def inverse_root(s):
-            stage[("inv", s)] = work.tile([P, SPAN], F32, name="inv", tag="inv", bufs=AHEAD + 1)
-            nc.scalar.activation(out=stage[("inv", s)][:], in_=stage[("den", s)][:], func=ACT.Abs_reciprocal_sqrt)
+            g, c, t = scores[s]
+            weighted_in = bank()
+            mx_pass(weighted_in, stationary(("input_weights", g, 0), t), ("inputs", 0, c), True, True)
+            divisors[s] = work.tile([P, SPAN], F32, name="divisor", tag="divisor", bufs=DIVISOR_TILES)
+            nc.scalar.activation(out=divisors[s][:], in_=weighted_in[:], func=ACT.Abs_reciprocal_sqrt)
 
         def square(s):
-            g, c, t = slots[s]
-            inv = stage[("inv", s)]
-            nc.scalar.activation(out=inv[:], in_=inv[:], func=ACT.Square, scale=column(0, g, t))
+            g, c, t = scores[s]
+            nc.scalar.activation(out=divisors[s][:], in_=divisors[s][:], func=ACT.Square, scale=column(VOTE, g, t))
+
+        def next_divisor(s):
+            if s < len(scores):
+                inverse_root(s)
+            if LEAD < s <= len(scores):
+                square(s - 1)
+
+        def weigh_outputs(s):
+            g, c, t = scores[s]
+            banks[("y", s)] = numerator_bank()
+            for h in range(HALVES):
+                mx_pass(banks[("y", s)], stationary(("U", g, h), t), ("outputs", h, c), h == 0, h == HALVES - 1)
 
         def score(s):
-            g, c, t = slots[s]
+            g, c, t = scores[s]
             if t == 0:
-                raw[("y", g, c)] = work.tile([P, PACK, SPAN], F32, name="y_rows", tag="y_rows", bufs=3)[:]
-            y = raw[("y", g, c)]
+                rows_of[("y", g, c)] = work.tile([P, SLOTS, SPAN], F32, name="y_rows", tag="y_rows", bufs=3)[:]
+            y = rows_of[("y", g, c)]
             nc.vector.scalar_tensor_tensor(
-                out=y[:, t, :], in0=stage[("num", s)][:], scalar=column(1, g, t),
-                in1=stage[("inv", s)][:], op0=ALU.add, op1=ALU.mult,
+                out=y[:, t, :], in0=banks[("y", s)][:], scalar=column(INTERCEPT, g, t),
+                in1=divisors[s][:], op0=ALU.add, op1=ALU.mult,
             )
-            rows = out_0[span(g), span(c)].rearrange("(p t) u -> p t u", t=PACK)
+            rows = out_0[span(g), span(c)].rearrange("(p t) u -> p t u", t=SLOTS)
             nc.sync.dma_start(out=rows[:, t, :], in_=y[:, t, :])
 
-        def quantise_scores(g, c):
+        def quantise_scores(piece):
+            g, c = piece[1:]
             codes = work.tile([P, SPAN], U32, name="y_codes", tag="y_codes", bufs=3, align_bytes=64)
-            nc.vector.quantize_mx(out=codes[:].bitcast(FP8X4), scales=y_scales[g][:, span(c)], in_=stage[("y", g, c)][:])
+            nc.vector.quantize_mx(out=codes[:].bitcast(FP8X4), scales=y_scales[g][:, span(c)], in_=staged[piece][:])
             nc.sync.dma_start(
                 out=out_1[g].rearrange("p m t -> p (m t)").bitcast(I32)[:, span(c)], in_=codes[:].bitcast(I32)
             )
@@ -277,123 +304,133 @@ def tile_cross_efficiency_composed_weights_k6_kernel(
                         in_=y_scales[g][32 * q : 32 * q + 4, :].bitcast(I32),
                     )
 
-        def il(key, n=0):
-            interleave(key, raw[key], n)
-
-        def den(s):
-            weigh_inputs(s)
-            inverse_root(s)
-
-        def turned(key):
-            turn(key)
-            turn_out(key, 0)
-            turn_out(key, 1)
-
-        def composed(g, h, t):
-            compose(g, h, t)
-            compose_out(g, h, t)
-
-        def weave(key, on_scalar=0):
-            if key[0] == "pn":
-                interleave_profiles(key[1], on_scalar // 32)
-            else:
-                il(key, on_scalar)
-
-        q = quantise
-        mn0, mo0, mo1, iw0 = ("mn", 0, 0), ("mo", 0, 0), ("mo", 0, 1), ("iw", 0, 0)
-        mn1, mo2, mo3, iw1 = ("mn", 1, 0), ("mo", 1, 0), ("mo", 1, 1), ("iw", 1, 0)
-        pn0, pn1 = ("pn", 0, 0), ("pn", 1, 0)
-        in0, in1, in2 = [("in", 0, c) for c in range(CHUNKS)]
+        weights = [("input_weights", g, 0) for g in range(GROUPS)]
+        now = [("mix_now", g, 0) for g in range(GROUPS)]
+        old = [[("mix_old", g, k) for k in range(HALVES)] for g in range(GROUPS)]
+        profiles = [("profiles_now", 0, h) for h in range(HALVES)]
+        unit_in = [("inputs", 0, c) for c in range(CHUNKS)]
+        unit_out = [[("outputs", h, c) for c in range(CHUNKS)] for h in range(HALVES)]
+        composed = [[("U", g, h) for h in range(HALVES)] for g in range(GROUPS)]
+        y_pieces = [("y", g, c) for g in range(GROUPS) for c in range(CHUNKS)]
 
         sort_vectors()
-        turned(iw0)
-        il(("in", 0, 0), HEAD)
+        turn(weights[0])
+        interleave(unit_in[0])
         turn_vectors()
-        q(("in", 0, 0))
-        q(iw0)
-        den(0)
-        den(1)
-        interleave_profiles(0, 0)
+        quantise(unit_in[0])
+        quantise(weights[0])
+        interleave_profiles(0, SLOTS - 1)
+        inverse_root(0)
+        inverse_root(1)
         square(0)
-        den(2)
-        square(1)
-        den(3)
-        turned(mn0)
-        q(("pn", 0, 0))
-        q(mn0)
-        sort_old_words()
-        sort_old_scales()
-        turned(mo0)
-        q(mo0)
-        turned(mo1)
-        interleave_profiles(1, 0)
-        q(mo1)
-        square(2)
+        turn(now[0])
+        for entry in LOADS[EARLY_LOADS:]:
+            load(*entry)
+        for s in (2, 3):
+            inverse_root(s)
+            square(s - 1)
         square(3)
-        il(("in", 0, 1))
-        q(("pn", 1, 0))
-        composed(0, 0, 0)
-        il(("out", 0, 0))
-        q(("in", 0, 1))
-        composed(0, 0, 1)
-        composed(0, 0, 2)
-        den(4)
-        composed(0, 0, 3)
-        il(("out", 1, 0))
-        q(("out", 0, 0))
-        den(5)
-        composed(0, 1, 0)
-        square(4)
-        il(("u", 0, 0))
-        q(("out", 1, 0))
-        composed(0, 1, 1)
-        square(5)
-        composed(0, 1, 2)
-        q(("u", 0, 0))
-        den(6)
-        composed(0, 1, 3)
-        den(7)
-        turned(mn1)
-        il(("out", 0, 1))
-        il(("u", 0, 1))
-        square(6)
-        square(7)
-        q(("out", 0, 1))
-        q(("u", 0, 1))
-        turned(mo2)
-        il(("out", 1, 1))
-        q(mn1)
-        turned(mo3)
+        interleave_profiles(1, SLOTS)
+        quantise(profiles[0])
+        interleave(unit_in[1])
+        quantise(now[0])
+        quantise(profiles[1])
+        quantise(unit_in[1])
 
-        extra = {
-            0: [lambda: q(("out", 1, 1)), lambda: il(("in", 0, 2))],
-            1: [lambda: q(mo2), lambda: q(("in", 0, 2)), lambda: il(("out", 0, 2), SHARE)],
-            2: [lambda: q(mo3), lambda: il(("out", 1, 2), SHARE)],
-            3: [lambda: turned(iw1), lambda: composed(1, 0, 0), lambda: q(("out", 0, 2))],
-            4: [lambda: composed(1, 0, 1), lambda: q(("out", 1, 2))],
-            5: [lambda: composed(1, 0, 2), lambda: composed(1, 0, 3), lambda: q(iw1)],
-            6: [lambda: composed(1, 1, 0), lambda: composed(1, 1, 1), lambda: il(("u", 1, 0))],
-            7: [lambda: composed(1, 1, 2), lambda: composed(1, 1, 3), lambda: q(("u", 1, 0))],
-            8: [lambda: il(("u", 1, 1))],
-            9: [lambda: q(("u", 1, 1))],
-        }
-        last = len(slots) - 1
-        weigh_outputs(0)
-        weigh_outputs(1)
-        for s in range(len(slots)):
-            g, c, t = slots[s]
-            if s + 2 <= last:
-                weigh_outputs(s + 2)
-            if 8 <= s + LEAD <= last:
-                den(s + LEAD)
-            if 8 <= s + LEAD - 1 <= last:
-                square(s + LEAD - 1)
+        for t in range(SLOTS):
+            compose_now(0, 0, t, numerator_bank)
+        inverse_root(4)
+        interleave(unit_in[2])
+        turn(old[0][0])
+        inverse_root(5)
+        turn(old[0][1])
+        sort_old_words()
+        quantise(unit_in[2])
+        sort_old_scales()
+        quantise(old[0][0])
+        inverse_root(6)
+        inverse_root(7)
+        for t in range(SLOTS):
+            compose_old(0, 0, t, 0)
+        quantise(old[0][1])
+        interleave(unit_out[0][0])
+        square(4)
+        for t in range(SLOTS):
+            compose_old(0, 0, t, 1)
+            add_floor(0, 0, t)
+        for c in (1, 2):
+            interleave(unit_out[0][c])
+            quantise(unit_out[0][c - 1])
+        interleave(composed[0][0])
+        for n, piece in enumerate((now[1], old[1][0])):
+            turn(piece)
+            for t in (2 * n, 2 * n + 1):
+                compose(0, 1, t)
+                if 5 + t < 2 * SLOTS:
+                    square(5 + t)
+        quantise(unit_out[0][2])
+        quantise(composed[0][0])
+        turn(old[1][1])
+
+        interleave(unit_out[1][0])
+        quantise(now[1])
+        quantise(old[1][0])
+        interleave(composed[0][1])
+        quantise(old[1][1])
+        quantise(unit_out[1][0])
+        quantise(composed[0][1])
+        inverse_root(8)
+        inverse_root(9)
+        turn(weights[1])
+        square(8)
+        square(9)
+        for t in (0, 1):
+            compose(1, 0, t)
+        for s in banks_of(0):
+            weigh_outputs(s)
+        staged[unit_out[1][1]] = shared_staging_tile()
+        interleave_runs(unit_out[1][1], 0, P, "vector")
+        quantise(weights[1])
+        quantise(unit_out[1][1])
+
+        last_of_group_0 = CHUNKS - 1
+        for j in range(rounds - 1):
+            shared = y_pieces[j - 1] if j > 0 else unit_out[1][2]
+            staged[shared] = shared_staging_tile()
+            interleave_runs(shared, 0, GPSIMD_RUNS, "gpsimd")
+            for s in banks_of(j):
+                score(s)
+            if j == 0:
+                for t in (2, 3):
+                    compose(1, 0, t)
+            for s in banks_of(j):
+                next_divisor(s + LEAD)
+                if j != last_of_group_0:
+                    weigh_outputs(s + SLOTS)
+            if j == 0:
+                for t in range(SLOTS):
+                    compose(1, 1, t)
+            half = {0: composed[1][0], last_of_group_0: composed[1][1]}.get(j)
+            if half:
+                interleave(half)
+            interleave_runs(shared, GPSIMD_RUNS, P - GPSIMD_RUNS, "vector")
+            if half:
+                quantise(half)
+            if j == last_of_group_0:
+                for s in banks_of(j + 1):
+                    weigh_outputs(s)
+            if j == 0:
+                quantise(shared)
+            else:
+                quantise_scores(shared)
+
+        before, final = y_pieces[-2], y_pieces[-1]
+        staged[before] = staging_tile()
+        interleave_runs(before, 0, P, "scalar")
+        for s in banks_of(rounds - 1):
             score(s)
-            for step in extra.get(s, []):
-                step()
-            if t == 0 and s > 0:
-                il(("y",) + slots[s - 1][:2], YSHARE if s > 8 else 0)
-            if t == 1 and s > 1:
-                quantise_scores(*slots[s - 2][:2])
-        il(("y", GROUPS - 1, CHUNKS - 1), 40)
-        quantise_scores(GROUPS - 1, CHUNKS - 1)
+        quantise_scores(before)
+        staged[final] = staging_tile()
+        interleave_runs(final, 0, P - LAST_SCALAR_RUNS, "vector")
+        interleave_runs(final, P - LAST_SCALAR_RUNS, LAST_SCALAR_RUNS, "scalar")
+        quantise_scores(final)

@@ -35,8 +35,9 @@ EARLY_LOADS = 8
 
 LEAD = 10
 DIVISOR_TILES = 13
-GPSIMD_RUNS = 72
-LAST_SCALAR_RUNS = 40
+GPSIMD_RUNS = 80
+LAST_GPSIMD_RUNS = 72
+LAST_SCALAR_RUNS = 48
 
 
 def tile_cross_efficiency_composed_weights_k6_kernel(
@@ -75,12 +76,12 @@ def tile_cross_efficiency_composed_weights_k6_kernel(
         def shared_staging_tile():
             return work.tile([P, WIDE], BF16, name="shared", tag="shared", bufs=1, align_bytes=64)
 
+        sorted_vectors = keep.tile([P, SPAN], F32, name="sorted_vectors")
+        nc.gpsimd.memset(sorted_vectors[:], 0.0)
         identity = keep.tile([P, P], F32, name="identity")
         make_identity(nc, identity[:])
         old_scale_rows = keep.tile([P, HALVES * R], U8, name="old_scale_rows")
         nc.gpsimd.memset(old_scale_rows[:].bitcast(I32), 0)
-        sorted_vectors = keep.tile([P, SPAN], F32, name="sorted_vectors")
-        nc.gpsimd.memset(sorted_vectors[:], 0.0)
 
         vectors = keep.tile([P, SPAN], BF16, name="vectors")
         for n, vector in ((VOTE, vote), (INTERCEPT, intercept), (FLOOR, floor_weight)):
@@ -195,18 +196,19 @@ def tile_cross_efficiency_composed_weights_k6_kernel(
         def column(n, g, t):
             return columns[:, t, n, g : g + 1]
 
+        by_slot = vectors[:].rearrange("p (c t) -> p t c", t=SLOTS)
+        slot_rows = sorted_vectors[:].rearrange("p (t c) -> p t c", t=SLOTS)
+        votes, intercepts, floors = [slice(32 * n, 32 * n + 2) for n in (VOTE, INTERCEPT, FLOOR)]
+
         def sort_vectors():
-            by_slot = vectors[:].rearrange("p (c t) -> p t c", t=SLOTS)
             by_run = vectors[:].rearrange("p (a t j) -> p t a j", t=SLOTS, j=4)
-            slot_rows = sorted_vectors[:].rearrange("p (t c) -> p t c", t=SLOTS)
             run_rows = sorted_vectors[:].rearrange("p (t a j) -> p t a j", t=SLOTS, j=4)
-            votes, intercepts, floors = [slice(32 * n, 32 * n + 2) for n in (VOTE, INTERCEPT, FLOOR)]
             nc.scalar.activation(out=slot_rows[votes], in_=by_slot[votes], func=ACT.Abs_reciprocal_sqrt)
             nc.scalar.copy(out=slot_rows[intercepts], in_=by_slot[intercepts])
             nc.scalar.copy(out=run_rows[floors], in_=by_run[floors])
-            nc.vector.tensor_tensor(out=slot_rows[votes], in0=slot_rows[votes], in1=by_slot[votes], op=ALU.mult)
 
         def turn_vectors():
+            nc.vector.tensor_tensor(out=slot_rows[votes], in0=slot_rows[votes], in1=by_slot[votes], op=ALU.mult)
             turned = bank()
             for t in range(SLOTS):
                 nc.tensor.transpose(turned[:, part(t)], sorted_vectors[:, part(t)], identity[:])
@@ -272,11 +274,11 @@ def tile_cross_efficiency_composed_weights_k6_kernel(
             if LEAD < s <= len(scores):
                 square(s - 1)
 
-        def weigh_outputs(s):
+        def weigh_outputs(s, h):
             g, c, t = scores[s]
-            banks[("y", s)] = numerator_bank()
-            for h in range(HALVES):
-                mx_pass(banks[("y", s)], stationary(("U", g, h), t), ("outputs", h, c), h == 0, h == HALVES - 1)
+            if h == 0:
+                banks[("y", s)] = numerator_bank()
+            mx_pass(banks[("y", s)], stationary(("U", g, h), t), ("outputs", h, c), h == 0, h == HALVES - 1)
 
         def score(s):
             g, c, t = scores[s]
@@ -290,19 +292,23 @@ def tile_cross_efficiency_composed_weights_k6_kernel(
             rows = out_0[span(g), span(c)].rearrange("(p t) u -> p t u", t=SLOTS)
             nc.sync.dma_start(out=rows[:, t, :], in_=y[:, t, :])
 
-        def quantise_scores(piece):
+        def quantise_scores(piece, first, count):
             g, c = piece[1:]
-            codes = work.tile([P, SPAN], U32, name="y_codes", tag="y_codes", bufs=3, align_bytes=64)
-            nc.vector.quantize_mx(out=codes[:].bitcast(FP8X4), scales=y_scales[g][:, span(c)], in_=staged[piece][:])
-            nc.sync.dma_start(
-                out=out_1[g].rearrange("p m t -> p (m t)").bitcast(I32)[:, span(c)], in_=codes[:].bitcast(I32)
+            units = slice(c * SPAN + first, c * SPAN + first + count)
+            codes = work.tile([P, count], U32, name="y_codes", tag="y_codes", bufs=3, align_bytes=64)
+            nc.vector.quantize_mx(
+                out=codes[:].bitcast(FP8X4), scales=y_scales[g][:, units],
+                in_=staged[piece][:, first * SLOTS : (first + count) * SLOTS],
             )
-            if c == CHUNKS - 1:
-                for q in range(4):
-                    nc.sync.dma_start(
-                        out=out_2[g, 4 * q : 4 * q + 4, :].bitcast(I32),
-                        in_=y_scales[g][32 * q : 32 * q + 4, :].bitcast(I32),
-                    )
+            words = out_1[g].rearrange("p m t -> p (m t)").bitcast(I32)
+            nc.sync.dma_start(out=words[:, units], in_=codes[:].bitcast(I32))
+
+        def store_scales(g, queue):
+            for q in range(4):
+                queue.dma_start(
+                    out=out_2[g, 4 * q : 4 * q + 4, :].bitcast(I32),
+                    in_=y_scales[g][32 * q : 32 * q + 4, :].bitcast(I32),
+                )
 
         weights = [("input_weights", g, 0) for g in range(GROUPS)]
         now = [("mix_now", g, 0) for g in range(GROUPS)]
@@ -379,6 +385,8 @@ def tile_cross_efficiency_composed_weights_k6_kernel(
         quantise(old[1][1])
         quantise(unit_out[1][0])
         quantise(composed[0][1])
+        for s in banks_of(0):
+            weigh_outputs(s, 0)
         inverse_root(8)
         inverse_root(9)
         turn(weights[1])
@@ -387,7 +395,7 @@ def tile_cross_efficiency_composed_weights_k6_kernel(
         for t in (0, 1):
             compose(1, 0, t)
         for s in banks_of(0):
-            weigh_outputs(s)
+            weigh_outputs(s, 1)
         staged[unit_out[1][1]] = shared_staging_tile()
         interleave_runs(unit_out[1][1], 0, P, "vector")
         quantise(weights[1])
@@ -405,8 +413,9 @@ def tile_cross_efficiency_composed_weights_k6_kernel(
                     compose(1, 0, t)
             for s in banks_of(j):
                 next_divisor(s + LEAD)
+                weigh_outputs(s + SLOTS, 0)
                 if j != last_of_group_0:
-                    weigh_outputs(s + SLOTS)
+                    weigh_outputs(s + SLOTS, 1)
             if j == 0:
                 for t in range(SLOTS):
                     compose(1, 1, t)
@@ -418,19 +427,24 @@ def tile_cross_efficiency_composed_weights_k6_kernel(
                 quantise(half)
             if j == last_of_group_0:
                 for s in banks_of(j + 1):
-                    weigh_outputs(s)
+                    weigh_outputs(s, 1)
             if j == 0:
                 quantise(shared)
             else:
-                quantise_scores(shared)
+                quantise_scores(shared, 0, SPAN)
+            if j == last_of_group_0 + 1:
+                store_scales(0, nc.sync)
 
         before, final = y_pieces[-2], y_pieces[-1]
-        staged[before] = staging_tile()
-        interleave_runs(before, 0, P, "scalar")
+        staged[before] = shared_staging_tile()
+        interleave_runs(before, 0, LAST_GPSIMD_RUNS, "gpsimd")
+        interleave_runs(before, LAST_GPSIMD_RUNS, P - LAST_GPSIMD_RUNS, "scalar")
         for s in banks_of(rounds - 1):
             score(s)
-        quantise_scores(before)
+        quantise_scores(before, 0, SPAN)
         staged[final] = staging_tile()
         interleave_runs(final, 0, P - LAST_SCALAR_RUNS, "vector")
         interleave_runs(final, P - LAST_SCALAR_RUNS, LAST_SCALAR_RUNS, "scalar")
-        quantise_scores(final)
+        for first in (0, SPAN // 2):
+            quantise_scores(final, first, SPAN // 2)
+        store_scales(GROUPS - 1, nc.scalar)

@@ -28,14 +28,14 @@ VOTE, INTERCEPT, FLOOR = 0, 1, 2
 
 LOADS = [
     ("input_weights", 0, 0, 1), ("inputs", 0, 0, 1), ("profiles_now", 0, 0, 2), ("mix_now", 0, 0, 1),
-    ("inputs", 0, 1, 2), ("profiles_old", 0, 0, 1), ("mix_old", 0, 0, 2), ("outputs", 0, 0, 3),
+    ("inputs", 0, 1, 2), ("mix_old", 0, 0, 2), ("profiles_old", 0, 0, 1), ("outputs", 0, 0, 3),
     ("mix_now", 1, 0, 1), ("mix_old", 1, 0, 2), ("outputs", 1, 0, 3), ("input_weights", 1, 0, 1),
 ]
 EARLY_LOADS = 8
 
 LEAD = 10
 DIVISOR_TILES = 13
-GPSIMD_RUNS = 80
+GPSIMD_RUNS = 84
 LAST_GPSIMD_RUNS = 72
 LAST_SCALAR_RUNS = 48
 
@@ -411,27 +411,31 @@ def tile_cross_efficiency_composed_weights_k6_kernel(
             if j == 0:
                 for t in (2, 3):
                     compose(1, 0, t)
+            numerators_each = 2 if j == 1 else 1
+            waiting = list(banks_of(j + 1))
             for s in banks_of(j):
                 next_divisor(s + LEAD)
-                weigh_outputs(s + SLOTS, 0)
-                if j != last_of_group_0:
-                    weigh_outputs(s + SLOTS, 1)
+                for later in waiting[:numerators_each]:
+                    weigh_outputs(later, 0)
+                    if j != last_of_group_0:
+                        weigh_outputs(later, 1)
+                waiting = waiting[numerators_each:]
             if j == 0:
                 for t in range(SLOTS):
                     compose(1, 1, t)
-            half = {0: composed[1][0], last_of_group_0: composed[1][1]}.get(j)
-            if half:
-                interleave(half)
+            if j == last_of_group_0:
+                interleave(composed[1][1])
             interleave_runs(shared, GPSIMD_RUNS, P - GPSIMD_RUNS, "vector")
-            if half:
-                quantise(half)
+            if j == 0:
+                interleave(composed[1][0])
+                quantise(shared)
+                continue
+            if j <= last_of_group_0:
+                quantise(composed[1][j - 1])
             if j == last_of_group_0:
                 for s in banks_of(j + 1):
                     weigh_outputs(s, 1)
-            if j == 0:
-                quantise(shared)
-            else:
-                quantise_scores(shared, 0, SPAN)
+            quantise_scores(shared, 0, SPAN)
             if j == last_of_group_0 + 1:
                 store_scales(0, nc.sync)
 

from contextlib import ExitStack

import concourse.mybir as mybir
from concourse.masks import make_identity

D, UNITS, KN, KO, R, I = 1024, 1536, 512, 1024, 1024, 512
FLOPS = 2 * D * R * (KN + KO) + 2 * D * UNITS * (R + I)

F32 = mybir.dt.float32
BF16 = mybir.dt.bfloat16
I32 = mybir.dt.int32
U32 = mybir.dt.uint32
U8 = mybir.dt.uint8
FP8X4 = mybir.dt.float8_e4m3fn_x4
FP4X4 = mybir.dt.float4_e2m1fn_x4
ACT = mybir.ActivationFunctionType
ALU = mybir.AluOpType

P = 128
SLOTS = 4
RUN = 4
SPAN = P * SLOTS
WIDE = SPAN * SLOTS
GROUPS = D // SPAN
HALVES = R // SPAN
CHUNKS = UNITS // SPAN
VOTE, INTERCEPT, FLOOR = 0, 1, 2

LOADS = [
    ("input_weights", 0, 0, 1), ("inputs", 0, 0, 1), ("profiles_now", 0, 0, 2), ("mix_now", 0, 0, 1),
    ("inputs", 0, 1, 2), ("mix_old", 0, 0, 2), ("profiles_old", 0, 0, 1), ("outputs", 0, 0, 3),
    ("mix_now", 1, 0, 1), ("mix_old", 1, 0, 2), ("outputs", 1, 0, 3), ("input_weights", 1, 0, 1),
]
EARLY_LOADS = 8

LEAD = 10
DIVISOR_TILES = 13
GPSIMD_RUNS = 84
LAST_GPSIMD_RUNS = 72
LAST_SCALAR_RUNS = 48


def tile_cross_efficiency_composed_weights_k6_kernel(
    tc, mix_now, profiles_now, mix_old, old_words, old_scales, floor_weight,
    outputs, input_weights, inputs, intercept, vote, out_0, out_1, out_2,
):
    nc = tc.nc
    with ExitStack() as ctx:
        keep = ctx.enter_context(tc.tile_pool(name="keep", bufs=1))
        work = ctx.enter_context(tc.tile_pool(name="work", bufs=2))
        psum = ctx.enter_context(tc.psum_pool(name="psum", bufs=4))
        ctx.enter_context(tc.manual_schedule())

        def span(i):
            return slice(i * SPAN, (i + 1) * SPAN)

        def part(i):
            return slice(i * P, (i + 1) * P)

        def bank():
            return psum.tile([P, SPAN], F32, name="bank", tag="bank")

        def numerator_bank():
            return psum.tile([P, SPAN], F32, name="numerator", tag="numerator")

        rows_of = {}
        words_of = {}
        staged = {}
        packed = {}
        banks = {}
        divisors = {}

        def staging_tile():
            return work.tile([P, WIDE], BF16, name="staged", tag="staged", bufs=5, align_bytes=64)

        def shared_staging_tile():
            return work.tile([P, WIDE], BF16, name="shared", tag="shared", bufs=1, align_bytes=64)

        sorted_vectors = keep.tile([P, SPAN], F32, name="sorted_vectors")
        nc.gpsimd.memset(sorted_vectors[:], 0.0)
        identity = keep.tile([P, P], F32, name="identity")
        make_identity(nc, identity[:])
        old_scale_rows = keep.tile([P, HALVES * R], U8, name="old_scale_rows")
        nc.gpsimd.memset(old_scale_rows[:].bitcast(I32), 0)

        vectors = keep.tile([P, SPAN], BF16, name="vectors")
        for n, vector in ((VOTE, vote), (INTERCEPT, intercept), (FLOOR, floor_weight)):
            nc.sync.dma_start(out=vectors[32 * n : 32 * n + 2, :], in_=vector.rearrange("(g c) -> g c", g=2))

        old_word_rows = keep.tile([P, HALVES * 2 * R], U8, name="old_word_rows")

        def load_old_profiles():
            nc.sync.dma_start(
                out=old_word_rows[:].bitcast(I32).rearrange("p (k w) -> p k w", k=HALVES),
                in_=old_words.bitcast(I32).rearrange("k p w -> p k w"),
            )
            for q in range(4):
                nc.sync.dma_start(
                    out=old_scale_rows[32 * q : 32 * q + 4, :].bitcast(I32).rearrange("p (k w) -> p k w", k=HALVES),
                    in_=old_scales.bitcast(I32)[:, 4 * q : 4 * q + 4, :].rearrange("k r w -> r k w"),
                )

        row_blocks = {"mix_now": mix_now, "mix_old": mix_old, "input_weights": input_weights, "inputs": inputs,
                      "profiles_now": profiles_now, "outputs": outputs}

        def load(operand, i, j, count):
            if operand == "profiles_old":
                load_old_profiles()
                return
            rows = row_blocks[operand][span(i), j * SPAN : (j + count) * SPAN]
            label = "load_%s_%d_%d" % (operand, i, j)
            tag = "load_" + operand if operand in ("mix_now", "input_weights") else label
            loaded = keep.tile([P, count * WIDE], BF16, name=label, tag=tag)
            view = loaded[:].rearrange("p (t c) -> p t c", t=SLOTS)
            if operand == "outputs":
                runs = rows.rearrange("(a t j) u -> t a j u", t=SLOTS, j=4)
                for t in range(SLOTS):
                    nc.sync.dma_start(out=view[:, t, :], in_=runs[t])
            else:
                nc.sync.dma_start(out=view, in_=rows.rearrange("(p t) c -> p t c", t=SLOTS))
            for n in range(count):
                rows_of[(operand, i, j + n)] = view[:, :, span(n)]
                words_of[(operand, i, j + n)] = (loaded[:].bitcast(F32), count * SPAN // 2, n * SPAN // 2)

        for entry in LOADS[:EARLY_LOADS]:
            load(*entry)

        def interleave_runs(piece, first, count, engine):
            if engine == "gpsimd":
                taken = slice(RUN * first, RUN * (first + count))
                nc.gpsimd.tensor_scalar(
                    out=staged[piece][:].rearrange("p (w t) -> p w t", t=SLOTS)[:, taken],
                    in0=rows_of[piece].rearrange("p t w -> p w t")[:, taken],
                    scalar1=1.0, scalar2=0.0, op0=ALU.mult, op1=ALU.add,
                )
                return
            dst = staged[piece][:].rearrange("p (c i t) -> p c t i", i=RUN, t=SLOTS)[:, first : first + count]
            src = rows_of[piece].rearrange("p t (c i) -> p c t i", i=RUN)[:, first : first + count]
            if engine == "scalar":
                nc.scalar.copy(out=dst, in_=src)
            else:
                nc.vector.tensor_copy(out=dst, in_=src)

        def interleave(piece):
            staged[piece] = staging_tile()
            interleave_runs(piece, 0, P, "vector")

        def interleave_profiles(h, vector_slots):
            piece = ("profiles_now", 0, h)
            staged[piece] = staging_tile()
            dst = staged[piece][:].rearrange("p (s a i t) -> p a s t i", s=SLOTS, i=4, t=SLOTS)
            src = rows_of[piece].rearrange("p t (a s i) -> p a s t i", s=SLOTS, i=4)
            nc.vector.tensor_copy(out=dst[:, :, :vector_slots], in_=src[:, :, :vector_slots])
            if vector_slots < SLOTS:
                nc.scalar.copy(out=dst[:, :, vector_slots:], in_=src[:, :, vector_slots:])

        def turn(piece):
            staged[piece] = staging_tile()
            pairs, pitch, first = words_of[piece]
            turned = [bank(), bank()]
            for t in range(SLOTS):
                for u in range(2):
                    start = pitch * t + first
                    nc.tensor.transpose(
                        turned[t // 2][:, part(2 * (t % 2) + u)], pairs[:, start + u : start + 2 * P : 2], identity[:]
                    )
            for n in range(2):
                nc.scalar.copy(
                    out=staged[piece][:].bitcast(F32)[:, span(n)].rearrange("p (s d u) -> p s d u", s=2, u=2),
                    in_=turned[n][:].rearrange("p (s u d) -> p s d u", s=2, u=2),
                )

        def quantise(piece):
            codes = keep.tile([P, SPAN], U32, name="codes_%s_%d_%d" % piece, align_bytes=64)
            scales = keep.tile([P, SPAN], U8, name="scales_%s_%d_%d" % piece, align_bytes=64)
            nc.vector.quantize_mx(out=codes[:].bitcast(FP8X4), scales=scales[:], in_=staged[piece][:])
            packed[piece] = (codes, scales)

        old_codes = keep.tile([P, HALVES * 2 * R], U8, name="old_codes", align_bytes=64)
        old_plane = keep.tile([P, HALVES * R], U8, name="old_plane", align_bytes=64)

        def sort_old_words():
            nc.vector.tensor_copy(
                out=old_codes[:].bitcast(I32).rearrange("p (x s a w) -> p x s a w", x=4, s=SLOTS, w=2),
                in_=old_word_rows[:].bitcast(I32).rearrange("p (x a s w) -> p x s a w", x=4, s=SLOTS, w=2),
            )

        def sort_old_scales():
            nc.vector.tensor_copy(
                out=old_plane[:].bitcast(I32).rearrange("p (x s a) -> p x s a", x=4, s=SLOTS),
                in_=old_scale_rows[:].bitcast(I32).rearrange("p (x a s) -> p x s a", x=4, s=SLOTS),
            )

        columns = keep.tile([P, SLOTS, 3, 2], F32, name="columns")

        def column(n, g, t):
            return columns[:, t, n, g : g + 1]

        by_slot = vectors[:].rearrange("p (c t) -> p t c", t=SLOTS)
        slot_rows = sorted_vectors[:].rearrange("p (t c) -> p t c", t=SLOTS)
        votes, intercepts, floors = [slice(32 * n, 32 * n + 2) for n in (VOTE, INTERCEPT, FLOOR)]

        def sort_vectors():
            by_run = vectors[:].rearrange("p (a t j) -> p t a j", t=SLOTS, j=4)
            run_rows = sorted_vectors[:].rearrange("p (t a j) -> p t a j", t=SLOTS, j=4)
            nc.scalar.activation(out=slot_rows[votes], in_=by_slot[votes], func=ACT.Abs_reciprocal_sqrt)
            nc.scalar.copy(out=slot_rows[intercepts], in_=by_slot[intercepts])
            nc.scalar.copy(out=run_rows[floors], in_=by_run[floors])

        def turn_vectors():
            nc.vector.tensor_tensor(out=slot_rows[votes], in0=slot_rows[votes], in1=by_slot[votes], op=ALU.mult)
            turned = bank()
            for t in range(SLOTS):
                nc.tensor.transpose(turned[:, part(t)], sorted_vectors[:, part(t)], identity[:])
            nc.scalar.copy(
                out=columns[:], in_=turned[:].rearrange("p (t n r) -> p t n r", t=SLOTS, r=32)[:, :, 0:3, 0:2]
            )

        def stationary(piece, t):
            codes, scales = packed[piece]
            return codes[:, part(t)].bitcast(FP8X4), scales[:, part(t)]

        def mx_pass(acc, lhs, moving_piece, start, stop):
            codes, scales = packed[moving_piece]
            nc.tensor.matmul_mx(
                out=acc[:], lhsT=lhs[0], lhsT_scale=lhs[1],
                rhs=codes[:].bitcast(FP8X4), rhs_scale=scales[:], start=start, stop=stop,
            )

        def compose_now(g, h, t, new_bank):
            if t == 0:
                rows_of[("U", g, h)] = work.tile([P, SLOTS, SPAN], BF16, name="u_rows", tag="u_rows")[:]
            banks[("U", g, h, t)] = new_bank()
            mx_pass(banks[("U", g, h, t)], stationary(("profiles_now", 0, h), t), ("mix_now", g, 0), True, False)

        def compose_old(g, h, t, k):
            x = (HALVES * k + h) * SLOTS + t
            lhs = (old_codes[:, 2 * P * x : 2 * P * (x + 1)].bitcast(FP4X4), old_plane[:, part(x)])
            mx_pass(banks[("U", g, h, t)], lhs, ("mix_old", g, k), False, k == HALVES - 1)

        def add_floor(g, h, t):
            nc.scalar.activation(
                out=rows_of[("U", g, h)][:, t, :], in_=banks[("U", g, h, t)][:],
                func=ACT.Identity, bias=column(FLOOR, h, t),
            )

        def compose(g, h, t):
            compose_now(g, h, t, bank)
            for k in range(HALVES):
                compose_old(g, h, t, k)
            add_floor(g, h, t)

        scores = [(g, c, t) for g in range(GROUPS) for c in range(CHUNKS) for t in range(SLOTS)]
        rounds = len(scores) // SLOTS
        y_scales = [keep.tile([P, UNITS], U8, name="y_scales%d" % g, align_bytes=64) for g in range(GROUPS)]

        def banks_of(j):
            return range(SLOTS * j, SLOTS * (j + 1))

        def inverse_root(s):
            g, c, t = scores[s]
            weighted_in = bank()
            mx_pass(weighted_in, stationary(("input_weights", g, 0), t), ("inputs", 0, c), True, True)
            divisors[s] = work.tile([P, SPAN], F32, name="divisor", tag="divisor", bufs=DIVISOR_TILES)
            nc.scalar.activation(out=divisors[s][:], in_=weighted_in[:], func=ACT.Abs_reciprocal_sqrt)

        def square(s):
            g, c, t = scores[s]
            nc.scalar.activation(out=divisors[s][:], in_=divisors[s][:], func=ACT.Square, scale=column(VOTE, g, t))

        def next_divisor(s):
            if s < len(scores):
                inverse_root(s)
            if LEAD < s <= len(scores):
                square(s - 1)

        def weigh_outputs(s, h):
            g, c, t = scores[s]
            if h == 0:
                banks[("y", s)] = numerator_bank()
            mx_pass(banks[("y", s)], stationary(("U", g, h), t), ("outputs", h, c), h == 0, h == HALVES - 1)

        def score(s):
            g, c, t = scores[s]
            if t == 0:
                rows_of[("y", g, c)] = work.tile([P, SLOTS, SPAN], F32, name="y_rows", tag="y_rows", bufs=3)[:]
            y = rows_of[("y", g, c)]
            nc.vector.scalar_tensor_tensor(
                out=y[:, t, :], in0=banks[("y", s)][:], scalar=column(INTERCEPT, g, t),
                in1=divisors[s][:], op0=ALU.add, op1=ALU.mult,
            )
            rows = out_0[span(g), span(c)].rearrange("(p t) u -> p t u", t=SLOTS)
            nc.sync.dma_start(out=rows[:, t, :], in_=y[:, t, :])

        def quantise_scores(piece, first, count):
            g, c = piece[1:]
            units = slice(c * SPAN + first, c * SPAN + first + count)
            codes = work.tile([P, count], U32, name="y_codes", tag="y_codes", bufs=3, align_bytes=64)
            nc.vector.quantize_mx(
                out=codes[:].bitcast(FP8X4), scales=y_scales[g][:, units],
                in_=staged[piece][:, first * SLOTS : (first + count) * SLOTS],
            )
            words = out_1[g].rearrange("p m t -> p (m t)").bitcast(I32)
            nc.sync.dma_start(out=words[:, units], in_=codes[:].bitcast(I32))

        def store_scales(g, queue):
            for q in range(4):
                queue.dma_start(
                    out=out_2[g, 4 * q : 4 * q + 4, :].bitcast(I32),
                    in_=y_scales[g][32 * q : 32 * q + 4, :].bitcast(I32),
                )

        weights = [("input_weights", g, 0) for g in range(GROUPS)]
        now = [("mix_now", g, 0) for g in range(GROUPS)]
        old = [[("mix_old", g, k) for k in range(HALVES)] for g in range(GROUPS)]
        profiles = [("profiles_now", 0, h) for h in range(HALVES)]
        unit_in = [("inputs", 0, c) for c in range(CHUNKS)]
        unit_out = [[("outputs", h, c) for c in range(CHUNKS)] for h in range(HALVES)]
        composed = [[("U", g, h) for h in range(HALVES)] for g in range(GROUPS)]
        y_pieces = [("y", g, c) for g in range(GROUPS) for c in range(CHUNKS)]

        sort_vectors()
        turn(weights[0])
        interleave(unit_in[0])
        turn_vectors()
        quantise(unit_in[0])
        quantise(weights[0])
        interleave_profiles(0, SLOTS - 1)
        inverse_root(0)
        inverse_root(1)
        square(0)
        turn(now[0])
        for entry in LOADS[EARLY_LOADS:]:
            load(*entry)
        for s in (2, 3):
            inverse_root(s)
            square(s - 1)
        square(3)
        interleave_profiles(1, SLOTS)
        quantise(profiles[0])
        interleave(unit_in[1])
        quantise(now[0])
        quantise(profiles[1])
        quantise(unit_in[1])

        for t in range(SLOTS):
            compose_now(0, 0, t, numerator_bank)
        inverse_root(4)
        interleave(unit_in[2])
        turn(old[0][0])
        inverse_root(5)
        turn(old[0][1])
        sort_old_words()
        quantise(unit_in[2])
        sort_old_scales()
        quantise(old[0][0])
        inverse_root(6)
        inverse_root(7)
        for t in range(SLOTS):
            compose_old(0, 0, t, 0)
        quantise(old[0][1])
        interleave(unit_out[0][0])
        square(4)
        for t in range(SLOTS):
            compose_old(0, 0, t, 1)
            add_floor(0, 0, t)
        for c in (1, 2):
            interleave(unit_out[0][c])
            quantise(unit_out[0][c - 1])
        interleave(composed[0][0])
        for n, piece in enumerate((now[1], old[1][0])):
            turn(piece)
            for t in (2 * n, 2 * n + 1):
                compose(0, 1, t)
                if 5 + t < 2 * SLOTS:
                    square(5 + t)
        quantise(unit_out[0][2])
        quantise(composed[0][0])
        turn(old[1][1])

        interleave(unit_out[1][0])
        quantise(now[1])
        quantise(old[1][0])
        interleave(composed[0][1])
        quantise(old[1][1])
        quantise(unit_out[1][0])
        quantise(composed[0][1])
        for s in banks_of(0):
            weigh_outputs(s, 0)
        inverse_root(8)
        inverse_root(9)
        turn(weights[1])
        square(8)
        square(9)
        for t in (0, 1):
            compose(1, 0, t)
        for s in banks_of(0):
            weigh_outputs(s, 1)
        staged[unit_out[1][1]] = shared_staging_tile()
        interleave_runs(unit_out[1][1], 0, P, "vector")
        quantise(weights[1])
        quantise(unit_out[1][1])

        last_of_group_0 = CHUNKS - 1
        for j in range(rounds - 1):
            shared = y_pieces[j - 1] if j > 0 else unit_out[1][2]
            staged[shared] = shared_staging_tile()
            interleave_runs(shared, 0, GPSIMD_RUNS, "gpsimd")
            for s in banks_of(j):
                score(s)
            if j == 0:
                for t in (2, 3):
                    compose(1, 0, t)
            numerators_each = 2 if j == 1 else 1
            waiting = list(banks_of(j + 1))
            for s in banks_of(j):
                next_divisor(s + LEAD)
                for later in waiting[:numerators_each]:
                    weigh_outputs(later, 0)
                    if j != last_of_group_0:
                        weigh_outputs(later, 1)
                waiting = waiting[numerators_each:]
            if j == 0:
                for t in range(SLOTS):
                    compose(1, 1, t)
            if j == last_of_group_0:
                interleave(composed[1][1])
            interleave_runs(shared, GPSIMD_RUNS, P - GPSIMD_RUNS, "vector")
            if j == 0:
                interleave(composed[1][0])
                quantise(shared)
                continue
            if j <= last_of_group_0:
                quantise(composed[1][j - 1])
            if j == last_of_group_0:
                for s in banks_of(j + 1):
                    weigh_outputs(s, 1)
            quantise_scores(shared, 0, SPAN)
            if j == last_of_group_0 + 1:
                store_scales(0, nc.sync)

        before, final = y_pieces[-2], y_pieces[-1]
        staged[before] = shared_staging_tile()
        interleave_runs(before, 0, LAST_GPSIMD_RUNS, "gpsimd")
        interleave_runs(before, LAST_GPSIMD_RUNS, P - LAST_GPSIMD_RUNS, "scalar")
        for s in banks_of(rounds - 1):
            score(s)
        quantise_scores(before, 0, SPAN)
        staged[final] = staging_tile()
        interleave_runs(final, 0, P - LAST_SCALAR_RUNS, "vector")
        interleave_runs(final, P - LAST_SCALAR_RUNS, LAST_SCALAR_RUNS, "scalar")
        for first in (0, SPAN // 2):
            quantise_scores(final, first, SPAN // 2)
        store_scales(GROUPS - 1, nc.scalar)
